import numpy as np, ml_dtypes
CORES = [9,25,41,57]
N = 4
BF = ml_dtypes.bfloat16
def gentries(a):
    return np.ascontiguousarray(a.reshape(8, 16, -1).transpose(0, 2, 1)).reshape(8, -1)
def gtable(e):
    e = np.asarray(e); return np.ascontiguousarray(e.reshape(8, -1, 16).transpose(0, 2, 1)).reshape(128, -1).astype(np.int32)
H, E, L = 2048, 32, 3
M = (N - 1) * E
def slot(r, q):
    return q - (1 if q > r else 0)
def flat(a):
    return np.ascontiguousarray(np.asarray(a).astype(np.int64).transpose(1, 0, 2)).reshape(8, -1)
def perms(rng):
    return np.argsort(rng.random((N, 8, H)), axis=-1)
def mesh(c, w, lens):
    nx, pv, tw = np.empty((N, 8, H), np.int64), np.empty((N, 8, H), np.int64), np.empty((N, 8, H), np.int64)
    for r in range(N):
        for g in range(8):
            e = np.add.accumulate(lens[r, g]); e = np.append(e[e < H], H); s = np.append(0, e[:-1])
            k = np.arange(1, H + 1); k[e - 1] = s; a = w[r, g]
            nx[r, g, a] = H * r + a[k]; pv[r, g, a[k]] = H * r + a
            b = c[r, g, M:].reshape(-1, 2); tw[r, g, b] = H * r + b[:, ::-1]
            for q in range(N):
                if q != r:
                    i, j = E * slot(r, q), E * slot(q, r)
                    tw[r, g, c[r, g, i:i + E]] = H * q + c[q, g, j:j + E]
    return {"nxt": nx.astype(np.int32), "prv": pv.astype(np.int32), "twn": tw.astype(np.int32), "far": np.stack([gtable(c[r, :, :M]) for r in range(N)])}
def draw(v, c, w, lens):
    d = {"x": v.astype(np.float32).astype(BF)}; d.update(mesh(c, w, lens)); return d
def setup_inputs(rng):
    v = rng.integers(-31, 32, (N, 128, H))
    return draw(v, perms(rng), perms(rng), rng.integers(3, 9, (N, 8, H)))
def setup_inputs_long(rng):
    v = rng.integers(-31, 32, (N, 128, H)); k = (np.arange(N)[:, None] + np.arange(8) + rng.integers(0, 3)) % 3
    lens = rng.integers(1, 3, (N, 8, H)); lens[k == 0] = H
    lens = np.where((k == 2)[:, :, None], rng.integers(1, 201, (N, 8, H)), lens)
    return draw(v, perms(rng), perms(rng), lens)
def setup_inputs_near(rng):
    v = np.where(rng.random((N, 128, H)) < 0.875, 31, -31); a = np.arange(H)
    e = np.append(a[:M // 2], a[H - M // 2:]); mid = a[M // 2:H - M // 2]; c = np.empty((N, 8, H), np.int64); c[:, :, M:] = mid
    for r in range(N):
        for g in range(8): c[r, g, :M] = rng.permutation(e)
    w = np.broadcast_to(a, (N, 8, H))
    return draw(v, c, w, rng.integers(2, 6, (N, 8, H)))
def setup_inputs_hops(rng):
    v = rng.integers(-31, 32, (N, 128, H)); c = perms(rng); w = c.copy()
    for r in range(N):
        for g in range(4): w[r, g, :M] = rng.permutation(c[r, g, :M])
    return draw(v, c, w, rng.integers(3, 17, (N, 8, H)))
def setup_inputs_spread(rng):
    v = (rng.integers(-31, 32, (N, 128, H)) >> rng.integers(0, 5, (N, 1, H))) * (rng.random((N, 1, H)) > 0.0625)
    return draw(v, perms(rng), perms(rng), 2 ** rng.integers(0, 8, (N, 8, H)))
def check_inputs(d):
    bad = []
    try:
        v = np.asarray(d["x"]).astype(np.float32)
        if not (v.shape == (N, 128, H) and np.isfinite(v).all() and (np.abs(v) <= 31).all() and (v == np.floor(v)).all()): bad.append("x: whole numbers from -31 to 31")
        nx, pv, tw = [np.asarray(d[k]).astype(np.int64) for k in ("nxt", "prv", "twn")]
        own = np.broadcast_to(np.arange(N)[:, None, None], (N, 8, H))
        if not all(a.shape == (N, 8, H) and (a >= 0).all() and (a < N * H).all() for a in (nx, pv, tw)): return bad + ["nxt, prv, twn: range"]
        if not ((nx // H == own).all() and (pv // H == own).all()): bad.append("nxt, prv: same rank")
        n, p, t = flat(nx), flat(pv), flat(tw); me = np.arange(N * H)
        if any((p[g][n[g]] != me).any() or (n[g][p[g]] != me).any() for g in range(8)): bad.append("nxt and prv: one undoes the other")
        if any((t[g][t[g]] != me).any() or (t[g] == me).any() for g in range(8)): bad.append("twn: pairs")
        for r in range(N):
            for q in range(N):
                if q != r and (np.sum(tw[r] // H == q, axis=1) != E).any(): bad.append("twn: E far twins a pair")
        f = np.stack([gentries(np.asarray(a).astype(np.int64)) for a in d["far"]])
        if not (f.shape == (N, 8, M) and (f >= 0).all() and (f < H).all()): return bad + ["far: range"]
        u = np.sort(f, axis=-1)
        if (u[..., 1:] == u[..., :-1]).any(): bad.append("far: all different")
        for r in range(N):
            for q in range(N):
                if q != r:
                    i, j = E * slot(r, q), E * slot(q, r)
                    if any((tw[r, g][f[r, g, i:i + E]] != H * q + f[q, g, j:j + E]).any() for g in range(8)): bad.append("far: order")
    except Exception:
        bad.append("shapes")
    return bad
def reference(x, nxt, prv, twn, far):
    v = x.astype(np.float32).reshape(N, 8, 16, H).transpose(1, 2, 0, 3).reshape(8, 16, N * H)
    n, p, t = flat(nxt), flat(prv), flat(twn)
    for k in range(L):
        W = v.shape[2]; v2 = np.empty((8, 16, 2 * W), np.float32); n2, p2 = np.empty((8, 2 * W), np.int64), np.empty((8, 2 * W), np.int64)
        for g in range(8):
            m = v[g] + v[g][:, n[g]]
            v2[g, :, 0::2] = m; v2[g, :, 1::2] = m[:, n[g]]
            n2[g, 0::2] = 2 * n[g]; n2[g, 1::2] = 2 * p[g][t[g]] + 1
            p2[g, 0::2] = 2 * p[g]; p2[g, 1::2] = 2 * t[g][n[g]] + 1
        v, n, p = v2, n2, p2; t = np.broadcast_to(np.arange(2 * W) ^ 1, (8, 2 * W))
    y = v.reshape(8, 16, N, -1)[..., 1::2].transpose(2, 0, 1, 3)
    return {"y": np.ascontiguousarray(y).reshape(N, 128, -1).astype(BF), "nx": np.ascontiguousarray(n.reshape(8, N, -1).transpose(1, 0, 2)).astype(np.float32)}

@@ -1,0 +1,294 @@
+from concourse.bass import DstId, RemoteDMATransfer
+from concourse.mybir import AluOpType, ActivationFunctionType
+
+H, E, N = 2048, 32, 4
+M = (N - 1) * E
+CHUNKS = [256, 256, 512, 512, 256, 256]
+
+SB = {"bfloat16": {"X": H, "X2": H, "A": H, "U": H, "At": H + M, "At2": H, "C": H, "K": H, "Ds": H + M, "Ds2": H, "M3": H + M,
+                   "Y": 4 * H, "oneb": 160, "Z0": 160, "Z1": 160, "Id": 128, "s1": M, "l1": M, "s2": 2 * M, "l2": 2 * M, "s3": M},
+      "float32": {"W": H, "SR": H, "TR": H, "F": 256, "HF": 128, "MS": 512, "NX": 1024, "mcol": 4, "ncol": 4, "J96": M, "K96": M,
+                  "onef": 160, "Zp": 160, "s0": M, "l0": M},
+      "int32": {"Mi": 384, "Hi": 128, "Hj": 128, "fari": 8, "mi": 4},
+      "uint16": {"L": 640, "FL": 8, "PFL": 8},
+      "float16": {"h16": 640}}
+SCRATCH = {nm: ("sbuf", [128, w], d) for d in SB for nm, w in SB[d].items()}
+SCRATCH["T16"] = ("sbuf", [128, 5, 128], "float16")
+for _nm in ("PL", "PF", "PG", "PH", "PM0", "PM1", "PM2", "PM3"):
+    SCRATCH[_nm] = ("psum", [128, 512], "float32")
+SEMAPHORES = (["ldM", "ldx", "ldf", "ldH", "ldP", "dSl", "dSg", "dTl", "dTg", "dUa", "dUb", "dDa", "dDb", "dAt", "out",
+               "r0", "r1", "r2", "r3", "q0", "q1", "q2", "q3",
+               "oneb", "onef", "W0", "Ath", "Hi", "Hj", "HF", "mi", "mcol", "ncol", "J96", "K96", "Z0", "Z1", "Zp", "Id",
+               "Wc", "F", "h0", "T0", "FL", "PL", "Ltn", "Lp", "s0", "s1", "SR", "SR1", "SR2", "Ca", "Cb", "hs", "Ts", "PF",
+               "PFL", "At0", "At1", "At2", "Atc", "Atp", "s2a", "s2c", "PS", "Ls", "Ds", "Dsp", "s3", "K", "ht", "Tt", "PT",
+               "Lu", "TR", "NX", "PH", "PM0", "PM1", "PM2", "PM3", "M3"]
+              + [nm + str(k) for nm in ("ldX", "A", "dA") for k in range(4)]
+              + ["yv%d" % k for k in range(len(CHUNKS))] + ["ys%d" % k for k in range(len(CHUNKS))])
+
+
+def rank_program(g, core, T, topo):
+    rank = T.rank_of(core)
+    if rank is None:
+        return
+    V, S, P, Q = g.vector, g.scalar, g.tensor, g.sync
+    add, sub, mul, mx, mn = AluOpType.add, AluOpType.subtract, AluOpType.mult, AluOpType.max, AluOpType.min
+    Copy, Ident = ActivationFunctionType.Copy, ActivationFunctionType.Identity
+    base = H * rank
+    total = {"ldM": 48, "ldx": 16, "ldf": 16, "ldH": 32, "ldP": 32, "dSl": 16, "dSg": 16, "dTl": 16, "dTg": 16,
+             "dUa": 16, "dUb": 16, "dDa": 16, "dDb": 16, "dAt": 32, "out": 16 * (len(CHUNKS) + 1),
+             "Wc": 3, "T0": 3, "K": 2, "NX": 8, "M3": 5, "Ca": 2, "Cb": 2}
+    for k in range(len(CHUNKS)):
+        total["yv%d" % k] = 2
+        total["ys%d" % k] = 2
+    for k in range(4):
+        total["r%d" % k] = 2 * (N - 1)
+        total["q%d" % k] = 2 * (N - 1)
+        for nm in ("ldX", "dA"):
+            total[nm + str(k)] = 16
+    allA = ["A%d" % k for k in range(4)]
+    quarter = [(512 * k, 512 * (k + 1)) for k in range(4)]
+    third = [(0, 768), (768, 1280), (1280, H)]
+
+    def wait(q, *names):
+        for nm in names:
+            q.wait_ge(T.sem[nm], total.get(nm, 1))
+
+    def done(ins, nm, n=1):
+        ins.then_inc(T.sem[nm], n)
+
+    def exchange(k, src, dst, off, w):
+        trs = []
+        for q in range(N):
+            if q == rank:
+                continue
+            i, j = q - (q > rank), rank - (rank > q)
+            rid, pid, _ = topo.addr(T.cores[q])
+            eng = topo.engines(core, T.cores[q])
+            trs.append(RemoteDMATransfer(dst_ids=[DstId(rid=rid, pnc=pid)], dma_engine_mask=(1 << eng[2 * i]) | (1 << eng[2 * i + 1]),
+                                         remote_sem=T.sem["r%d" % k], src=src[:, w * i:w * (i + 1)],
+                                         dst=dst[:, off + w * j:off + w * (j + 1)]))
+        g.remote_dma_fused(trs, local_sem=T.sem["q%d" % k])
+
+    Lt, Ln, Lp, Ls, Lu = 0, 128, 256, 384, 512
+    far, pf = T.FL[:, 0:6], T.PFL[:, 0:6]
+
+    def lst(c0, a=0, b=H):
+        return T.L[:, c0 + a // 16:c0 + b // 16]
+
+    def to_list(ps, t0, t1, ev):
+        nt = t1 - t0
+        for s in range(8):
+            b, u = s // 2, s % 2
+            z = T.Z1 if u else T.Z0
+            for g1 in range(2):
+                o = 16 - 16 * (g1 - u)
+                c = 32 * b + 16 * g1
+                rhs = T.T16[:, t0, c:c + 16] if nt == 1 else T.T16[:, t0:t1, c:c + 16]
+                ins = P.matmul(ps[:, s:128 * nt:8], z[:, o:o + 128], rhs, g1 == 0, g1 == 1)
+        done(ins, ev)
+
+    done(Q.dma_start(T.Mi[:, 0:128], T.twn[:]), "ldM", 16)
+    done(Q.dma_start(T.Mi[:, 128:256], T.nxt[:]), "ldM", 16)
+    done(Q.dma_start(T.Mi[:, 256:384], T.prv[:]), "ldM", 16)
+    done(Q.dma_start(T.X[:], T.x[:]), "ldx", 16)
+    done(Q.dma_start(T.X2[:, 0:512], T.x[:, 0:512]), "ldX0", 16)
+    wait(Q, "W0", "Wc", "F")
+    done(Q.dma_start(T.W[2::16, :], T.F[:, 128:256]), "ldP", 16)
+    done(Q.dma_start(T.W[3::16, :], T.F[:, 128:256]), "ldP", 16)
+    for k in (1, 2):
+        a, b = quarter[k]
+        done(Q.dma_start(T.X2[:, a:b], T.x[:, a:b]), "ldX%d" % k, 16)
+    for k, (a, b) in enumerate(quarter):
+        wait(Q, "A%d" % k)
+        done(Q.dma_start(T.U[:, a:b], T.A[:, a:b]), "dA%d" % k, 16)
+    wait(Q, "SR1")
+    done(Q.dma_start(T.MS[:, 0:128], T.SR[2::16, :]), "dSl", 16)
+    for k, (a, b) in enumerate(third[0:2]):
+        wait(Q, "At%d" % k)
+        done(Q.dma_start(T.At2[:, a:b], T.At[:, a:b]), "dAt", 16)
+    wait(Q, "SR2")
+    done(Q.dma_start(T.MS[:, 128:256], T.SR[3::16, :]), "dSg", 16)
+    wait(Q, "TR")
+    done(Q.dma_start(T.MS[:, 256:384], T.TR[0::16, :]), "dTl", 16)
+    done(Q.dma_start(T.MS[:, 384:512], T.TR[1::16, :]), "dTg", 16)
+    wait(Q, "Dsp")
+    done(Q.dma_start(T.Ds2[:, 0:1024], T.Ds[:, 0:1024]), "dDa", 16)
+    wait(Q, "q3")
+    done(Q.dma_start(T.Ds2[:, 1024:H], T.Ds[:, 1024:H]), "dDb", 16)
+    wait(Q, "NX")
+    done(Q.dma_start(T.nx[:], T.NX[:]), "out", 16)
+    a = 0
+    for k, w in enumerate(CHUNKS):
+        wait(Q, "yv%d" % k, "ys%d" % k)
+        done(Q.dma_start(T.y[:, 4 * a:4 * (a + w)], T.Y[:, 4 * a:4 * (a + w)]), "out", 16)
+        a += w
+    wait(Q, "out")
+
+    done(g.iota(T.Hi[:], [[1, 128]], 0, 128), "Hi")
+    wait(g, "oneb")
+    done(g.affine_select(T.Z0[:], T.oneb[:], [[32, 5], [1000, 2], [1, 16]], AluOpType.is_equal, 0.0, -1000, -1), "Z0")
+    done(g.affine_select(T.Z1[:], T.oneb[:], [[32, 5], [1000, 2], [1, 16]], AluOpType.is_equal, 0.0, -16, -1), "Z1")
+    done(g.iota(T.J96[:], [[1, M]], base + H, 0, allow_small_or_imprecise_dtypes=True), "J96")
+    done(g.dma_start(T.X2[:, 1536:H], T.x[:, 1536:H]), "ldX3", 16)
+    wait(g, "onef")
+    done(g.affine_select(T.Zp[:], T.onef[:], [[16, 10], [1001, 16]], AluOpType.is_equal, 0.0, -3016, -1), "Zp")
+    done(g.affine_select(T.Id[:], T.oneb[:, 0:128], [[-1, 128]], AluOpType.is_equal, 0.0, 0, 1), "Id")
+    wait(g, "s0")
+    exchange(0, T.s0, T.l0, 0, E)
+    wait(g, "s1")
+    exchange(1, T.s1, T.l1, 0, E)
+    wait(g, "Ca")
+    done(g.dma_start(T.U[:, 0:1024], T.C[:, 0:1024], accum_op=add), "dUa", 16)
+    wait(g, "s2a", "s2c")
+    exchange(2, T.s2, T.l2, 0, 2 * E)
+    wait(g, "Cb")
+    done(g.dma_start(T.U[:, 1024:H], T.C[:, 1024:H], accum_op=add), "dUb", 16)
+    wait(g, "s3")
+    exchange(3, T.s3, T.Ds, H, E)
+    wait(g, "q0", "q1", "q2")
+
+    wait(P, "T0", "Z0", "Z1")
+    to_list(T.PL, 0, 3, "PL")
+    wait(P, "s0", "Zp")
+    for i in range(16):
+        ins = P.matmul(T.PF[:, 0:6], T.Zp[:, 19 - i:147 - i], T.s0[:, i:M:16], i == 0, i == 15)
+    done(ins, "PF")
+    wait(P, "Ts")
+    to_list(T.PG, 3, 4, "PS")
+    wait(P, "Ca", "Cb", "Id")
+    for k, (a, b) in enumerate(quarter):
+        P.matmul(T["PM%d" % k][:], T.Id[:], T.C[:, a:b], True, False)
+    wait(P, "s1", "s2a", "r2")
+    P.matmul(T.PH[:, 0:M], T.Id[:], T.s1[:], True, False)
+    P.matmul(T.PH[:, 0:M], T.Id[:], T.s2[:, 0:2 * M:2], False, False)
+    done(P.matmul(T.PH[:, 0:M], T.Id[:], T.l2[:, 1:2 * M:2], False, True), "PH")
+    wait(P, "Dsp")
+    for k, (a, b) in enumerate(quarter):
+        done(P.matmul(T["PM%d" % k][:], T.Id[:], T.Ds[:, a:b], False, True), "PM%d" % k)
+    wait(P, "Tt", "Ls")
+    to_list(T.PG, 4, 5, "PT")
+
+    done(S.dma_start(T.fari[:, 0:6], T.far[:]), "ldf", 16)
+    wait(S, "W0")
+    for k in range(1, 4):
+        done(S.activation(T.W[:, 512 * k:512 * (k + 1)], T.W[:, 0:512], Copy), "Wc")
+    wait(S, "Wc", "HF")
+    done(S.dma_start(T.W[0::16, :], T.HF[:]), "ldH", 16)
+    done(S.dma_start(T.W[1::16, :], T.HF[:]), "ldH", 16)
+    wait(S, "ldH", "ldP", "FL", "mcol")
+    done(S.activation(T.s0[:], T.W[:].indirect(far), Ident, scale=T.mcol[:, 0:1]), "s0")
+    wait(S, "Ltn")
+    done(S.activation(T.SR[:], T.W[:].indirect(lst(Lt)), Copy), "SR")
+    wait(S, *allA)
+    for k, (a, b) in enumerate(third):
+        done(S.activation(T.At[:, a:b], T.A[:].indirect(lst(Lt, a, b)), Copy), "At%d" % k)
+    wait(S, "Ca", "Cb")
+    done(S.activation(T.s2[:, 1:2 * M:2], T.C[:].indirect(far), Copy), "s2c")
+    wait(S, "SR2")
+    done(S.activation(T.TR[:], T.SR[:].indirect(lst(Ln)), Copy), "TR")
+
+    def nxop(k, src, c):
+        done(S.activation(T.NX[:, k:1024:8], src, Ident, bias=float(c), scale=8.0), "NX")
+    nxop(0, T.F[:, 0:128], 0)
+    nxop(1, T.F[:, 0:128], 7)
+    nxop(3, T.F[:, 128:256], 1)
+    nxop(6, T.F[:, 128:256], 2)
+    wait(S, "dSg")
+    nxop(4, T.MS[:, 128:256], 4)
+    nxop(5, T.MS[:, 128:256], 3)
+    wait(S, "PH")
+    done(S.activation(T.M3[:, H:H + M], T.PH[:, 0:M], Copy), "M3")
+    for k, (a, b) in enumerate(quarter):
+        wait(S, "PM%d" % k)
+        done(S.activation(T.M3[:, a:b], T["PM%d" % k][:], Copy), "M3")
+    wait(S, "dTg")
+    nxop(2, T.MS[:, 384:512], 6)
+    nxop(7, T.MS[:, 384:512], 5)
+    wait(S, "K")
+    a = 0
+    for k, w in enumerate(CHUNKS):
+        b = a + w
+        done(S.activation(T.Y[:, 4 * a:4 * b:4], T.K[:].indirect(lst(Ln, a, b)), Copy), "ys%d" % k)
+        if k == 0:
+            wait(S, "M3", "Lu")
+        done(S.activation(T.Y[:, 4 * a + 1:4 * b:4], T.M3[:].indirect(lst(Lu, a, b)), Copy), "ys%d" % k)
+        a = b
+
+    done(V.memset(T.oneb[:], 1.0), "oneb")
+    done(V.memset(T.W[:, 0:512], 0.0), "W0")
+    done(V.memset(T.onef[:], 1.0), "onef")
+    done(V.memset(T.At[:, H:H + M], 0.0), "Ath")
+    wait(V, "Hi")
+    done(V.tensor_scalar(T.Hj[:], T.Hi[:], H - 1, None, AluOpType.bitwise_and), "Hj")
+    done(V.tensor_scalar(T.mi[:, 0:1], T.Hi[:, 0:1], 7, 1, AluOpType.logical_shift_right, AluOpType.bitwise_and), "mi")
+    wait(V, "Hj")
+    done(V.tensor_scalar(T.HF[:], T.Hj[:], float(base), None, add), "HF")
+    wait(V, "mi")
+    done(V.tensor_copy(T.mcol[:, 0:1], T.mi[:, 0:1]), "mcol")
+    done(V.tensor_scalar(T.ncol[:, 0:1], T.mi[:, 0:1], -1.0, 1.0, mul, add), "ncol")
+    wait(V, "ldM")
+    done(V.tensor_copy(T.F[:], T.Mi[:, 128:384]), "F")
+    done(V.tensor_scalar(T.h16[:, 0:384], T.Mi[:], float(base), float(H - 1), sub, mn), "h0")
+    wait(V, "h0")
+    for k in range(3):
+        done(V.transpose(T.T16[:, k, :], T.h16[:, 128 * k:128 * (k + 1)]), "T0")
+    wait(V, "ldf")
+    done(V.tensor_copy(far, T.fari[:, 0:6]), "FL")
+    wait(V, "J96", "ncol")
+    done(V.tensor_scalar(T.K96[:], T.J96[:], T.ncol[:, 0:1], None, mul), "K96")
+    wait(V, "PL")
+    done(V.tensor_copy(T.L[:, 0:256], T.PL[:, 0:256]), "Ltn")
+    wait(V, "Ltn", "ldx")
+    for k, (a, b) in enumerate(quarter):
+        wait(V, "ldX%d" % k)
+        done(V.tensor_tensor(T.A[:, a:b], T.X[:].indirect(lst(Ln, a, b)), T.X2[:, a:b], add), "A%d" % k)
+    wait(V, "FL", *allA)
+    done(V.tensor_copy(T.s1[:], T.A[:].indirect(far)), "s1")
+    wait(V, "SR", "K96")
+    done(V.tensor_copy(T.SR[:].indirect(far), T.K96[:]), "SR1")
+    for k, (a, b) in enumerate(quarter):
+        wait(V, "dA%d" % k)
+        done(V.tensor_tensor(T.C[:, a:b], T.A[:].indirect(lst(Ln, a, b)), T.U[:, a:b], add), "Ca" if k < 2 else "Cb")
+    wait(V, "dSl")
+    done(V.tensor_scalar(T.h16[:, 384:512], T.MS[:, 0:128], float(base + 1024), None, sub), "hs")
+    wait(V, "hs")
+    done(V.transpose(T.T16[:, 3, :], T.h16[:, 384:512]), "Ts")
+    wait(V, "PF")
+    done(V.tensor_scalar(pf, T.PF[:, 0:6], float(base), None, sub), "PFL")
+    wait(V, "r0", "SR1")
+    done(V.tensor_tensor(T.SR[:].indirect(far), T.l0[:], T.K96[:], mx), "SR2")
+    wait(V, "At2")
+    done(V.tensor_copy(T.At2[:, third[2][0]:H], T.At[:, third[2][0]:H]), "Atc")
+    wait(V, "r1", "dAt", "Atc")
+    done(V.tensor_copy(T.At[:, 0:H].indirect(far), T.l1[:]), "Atp")
+    wait(V, "Atp", "PFL")
+    done(V.tensor_copy(T.s2[:, 0:2 * M:2], T.At[:, 0:H].indirect(pf)), "s2a")
+    wait(V, "PS")
+    done(V.tensor_scalar(T.L[:, Ls:Ls + 128], T.PG[:, 0:128], 1024.0, None, add), "Ls")
+    wait(V, "Ls", "Ath")
+    done(V.tensor_tensor(T.Ds[:, 0:H], T.At[:].indirect(lst(Ls)), T.At2[:], add), "Ds")
+    done(V.tensor_copy(T.L[:, Lp:Lp + 128], T.PL[:, 256:384]), "Lp")
+    wait(V, "Ds", "r2")
+    done(V.tensor_tensor(T.Ds[:, 0:H].indirect(far), T.l1[:], T.l2[:, 0:2 * M:2], add), "Dsp")
+    wait(V, "Dsp")
+    done(V.tensor_copy(T.s3[:], T.Ds[:, 0:H].indirect(pf)), "s3")
+    wait(V, "dUa", "dUb")
+    done(V.tensor_tensor(T.K[:, 0:1024], T.U[:].indirect(lst(Ln, 0, 1024)), T.A[:, 0:1024], add), "K")
+    wait(V, "dTl")
+    done(V.tensor_scalar(T.h16[:, 512:640], T.MS[:, 256:384], float(base + 1024), None, sub), "ht")
+    wait(V, "ht")
+    done(V.transpose(T.T16[:, 4, :], T.h16[:, 512:640]), "Tt")
+    done(V.tensor_tensor(T.K[:, 1024:H], T.U[:].indirect(lst(Ln, 1024, H)), T.A[:, 1024:H], add), "K")
+    wait(V, "PT")
+    done(V.tensor_scalar(T.L[:, Lu:Lu + 128], T.PG[:, 0:128], 1024.0, None, add), "Lu")
+    wait(V, "Lp")
+    a = 0
+    for k, w in enumerate(CHUNKS):
+        b = a + w
+        done(V.tensor_tensor(T.Y[:, 4 * a + 3:4 * b:4], T.At[:, 0:H].indirect(lst(Lp, a, b)), T.U[:, a:b], add), "yv%d" % k)
+        if a == 0:
+            wait(V, "r3", "dDa")
+        if a == 1024:
+            wait(V, "dDb")
+        done(V.tensor_tensor(T.Y[:, 4 * a + 2:4 * b:4], T.Ds[:].indirect(lst(Ls, a, b)), T.Ds2[:, a:b], add), "yv%d" % k)
+        a = b

@@ -3,25 +3,28 @@ from concourse.mybir import AluOpType, ActivationFunctionType
 
 H, E, N = 2048, 32, 4
 M = (N - 1) * E
-CHUNKS = [256, 256, 512, 512, 256, 256]
+CHUNKS = [256, 512, 512, 384, 256, 128]
+KV = 1536
+LEAD = 1
 
-SB = {"bfloat16": {"X": H, "X2": H, "A": H, "U": H, "At": H + M, "At2": H, "C": H, "K": H, "Ds": H + M, "Ds2": H, "M3": H + M,
-                   "Y": 4 * H, "oneb": 160, "Z0": 160, "Z1": 160, "Id": 128, "s1": M, "l1": M, "s2": 2 * M, "l2": 2 * M, "s3": M},
-      "float32": {"W": H, "SR": H, "TR": H, "F": 256, "HF": 128, "MS": 512, "NX": 1024, "mcol": 4, "ncol": 4, "J96": M, "K96": M,
+SB = {"bfloat16": {"X": H, "X2": H, "A": H, "U": H, "At": H + M, "At2": H, "C": H, "K": H, "Un": H - KV, "Ds": H + M, "Ds2": H,
+                   "M3": H + M, "Y": 4 * H, "oneb": 160, "Z0": 160, "Z1": 160, "Id": 128,
+                   "s1": M, "l1": M, "s2": 2 * M, "l2": 2 * M, "s3": M},
+      "float32": {"W": H, "SR": H, "TR": H, "F": 256, "MS": 512, "NX": 1024, "mcol": 4, "ncol": 4, "J96": M, "K96": M,
                   "onef": 160, "Zp": 160, "s0": M, "l0": M},
-      "int32": {"Mi": 384, "Hi": 128, "Hj": 128, "fari": 8, "mi": 4},
+      "int32": {"Mi": 384, "pi": 4, "fari": 8, "mi": 4},
       "uint16": {"L": 640, "FL": 8, "PFL": 8},
       "float16": {"h16": 640}}
 SCRATCH = {nm: ("sbuf", [128, w], d) for d in SB for nm, w in SB[d].items()}
 SCRATCH["T16"] = ("sbuf", [128, 5, 128], "float16")
 for _nm in ("PL", "PF", "PG", "PH", "PM0", "PM1", "PM2", "PM3"):
     SCRATCH[_nm] = ("psum", [128, 512], "float32")
-SEMAPHORES = (["ldM", "ldx", "ldf", "ldH", "ldP", "dSl", "dSg", "dTl", "dTg", "dUa", "dUb", "dDa", "dDb", "dAt", "out",
+SEMAPHORES = (["ldM", "ldp", "ldx", "ldf", "ldP", "dSl", "dSg", "dTl", "dTg", "dUa", "dUb", "dDa", "dDb", "dAt", "out",
                "r0", "r1", "r2", "r3", "q0", "q1", "q2", "q3",
-               "oneb", "onef", "W0", "Ath", "Hi", "Hj", "HF", "mi", "mcol", "ncol", "J96", "K96", "Z0", "Z1", "Zp", "Id",
-               "Wc", "F", "h0", "T0", "FL", "PL", "Ltn", "Lp", "s0", "s1", "SR", "SR1", "SR2", "Ca", "Cb", "hs", "Ts", "PF",
+               "oneb", "onef", "W0", "W1", "Ath", "pi", "mi", "mcol", "ncol", "J96", "K96", "Z0", "Z1", "Zp", "Id",
+               "Wc", "F", "Fn", "h0", "T0", "FL", "PL", "Ltn", "Lp", "s0", "s1", "SR", "SR1", "SR2", "Ca", "Cb", "hs", "Ts", "PF",
                "PFL", "At0", "At1", "At2", "Atc", "Atp", "s2a", "s2c", "PS", "Ls", "Ds", "Dsp", "s3", "K", "ht", "Tt", "PT",
-               "Lu", "TR", "NX", "PH", "PM0", "PM1", "PM2", "PM3", "M3"]
+               "Lu", "TR", "NX", "PH", "PM0", "PM1", "PM2", "PM3", "M3", "Un", "PK", "Ke"]
               + [nm + str(k) for nm in ("ldX", "A", "dA") for k in range(4)]
               + ["yv%d" % k for k in range(len(CHUNKS))] + ["ys%d" % k for k in range(len(CHUNKS))])
 
@@ -34,9 +37,9 @@ def rank_program(g, core, T, topo):
     add, sub, mul, mx, mn = AluOpType.add, AluOpType.subtract, AluOpType.mult, AluOpType.max, AluOpType.min
     Copy, Ident = ActivationFunctionType.Copy, ActivationFunctionType.Identity
     base = H * rank
-    total = {"ldM": 48, "ldx": 16, "ldf": 16, "ldH": 32, "ldP": 32, "dSl": 16, "dSg": 16, "dTl": 16, "dTg": 16,
+    total = {"ldM": 32, "ldp": 16, "ldx": 16, "ldf": 16, "ldP": 32, "dSl": 16, "dSg": 16, "dTl": 16, "dTg": 16,
              "dUa": 16, "dUb": 16, "dDa": 16, "dDb": 16, "dAt": 32, "out": 16 * (len(CHUNKS) + 1),
-             "Wc": 3, "T0": 3, "K": 2, "NX": 8, "M3": 5, "Ca": 2, "Cb": 2}
+             "Wc": 4, "W1": 3, "T0": 3, "NX": 8, "M3": 5, "Ca": 2, "Cb": 2, "TR": 2}
     for k in range(len(CHUNKS)):
         total["yv%d" % k] = 2
         total["ys%d" % k] = 2
@@ -47,7 +50,8 @@ def rank_program(g, core, T, topo):
             total[nm + str(k)] = 16
     allA = ["A%d" % k for k in range(4)]
     quarter = [(512 * k, 512 * (k + 1)) for k in range(4)]
-    third = [(0, 768), (768, 1280), (1280, H)]
+    third = [(0, 768), (768, 1536), (1536, H)]
+    edges = [sum(CHUNKS[:k]) for k in range(len(CHUNKS) + 1)]
 
     def wait(q, *names):
         for nm in names:
@@ -58,13 +62,12 @@ def rank_program(g, core, T, topo):
 
     def exchange(k, src, dst, off, w):
         trs = []
-        for q in range(N):
-            if q == rank:
-                continue
+        for d in range(1, N):
+            q = (rank + d) % N
             i, j = q - (q > rank), rank - (rank > q)
             rid, pid, _ = topo.addr(T.cores[q])
-            eng = topo.engines(core, T.cores[q])
-            trs.append(RemoteDMATransfer(dst_ids=[DstId(rid=rid, pnc=pid)], dma_engine_mask=(1 << eng[2 * i]) | (1 << eng[2 * i + 1]),
+            eng = topo.engines(core, T.cores[q])[2 * d - 2:2 * d]
+            trs.append(RemoteDMATransfer(dst_ids=[DstId(rid=rid, pnc=pid)], dma_engine_mask=sum(1 << e for e in eng),
                                          remote_sem=T.sem["r%d" % k], src=src[:, w * i:w * (i + 1)],
                                          dst=dst[:, off + w * j:off + w * (j + 1)]))
         g.remote_dma_fused(trs, local_sem=T.sem["q%d" % k])
@@ -87,15 +90,14 @@ def rank_program(g, core, T, topo):
                 ins = P.matmul(ps[:, s:128 * nt:8], z[:, o:o + 128], rhs, g1 == 0, g1 == 1)
         done(ins, ev)
 
+    done(Q.dma_start(T.Mi[:, 256:384], T.prv[:]), "ldp", 16)
     done(Q.dma_start(T.Mi[:, 0:128], T.twn[:]), "ldM", 16)
     done(Q.dma_start(T.Mi[:, 128:256], T.nxt[:]), "ldM", 16)
-    done(Q.dma_start(T.Mi[:, 256:384], T.prv[:]), "ldM", 16)
     done(Q.dma_start(T.X[:], T.x[:]), "ldx", 16)
-    done(Q.dma_start(T.X2[:, 0:512], T.x[:, 0:512]), "ldX0", 16)
-    wait(Q, "W0", "Wc", "F")
+    wait(Q, "W0", "W1", "Wc", "F")
     done(Q.dma_start(T.W[2::16, :], T.F[:, 128:256]), "ldP", 16)
     done(Q.dma_start(T.W[3::16, :], T.F[:, 128:256]), "ldP", 16)
-    for k in (1, 2):
+    for k in (1, 2, 3):
         a, b = quarter[k]
         done(Q.dma_start(T.X2[:, a:b], T.x[:, a:b]), "ldX%d" % k, 16)
     for k, (a, b) in enumerate(quarter):
@@ -117,32 +119,31 @@ def rank_program(g, core, T, topo):
     done(Q.dma_start(T.Ds2[:, 1024:H], T.Ds[:, 1024:H]), "dDb", 16)
     wait(Q, "NX")
     done(Q.dma_start(T.nx[:], T.NX[:]), "out", 16)
-    a = 0
-    for k, w in enumerate(CHUNKS):
+    for k in range(len(CHUNKS)):
+        a, b = edges[k], edges[k + 1]
         wait(Q, "yv%d" % k, "ys%d" % k)
-        done(Q.dma_start(T.y[:, 4 * a:4 * (a + w)], T.Y[:, 4 * a:4 * (a + w)]), "out", 16)
-        a += w
+        done(Q.dma_start(T.y[:, 4 * a:4 * b], T.Y[:, 4 * a:4 * b]), "out", 16)
     wait(Q, "out")
 
-    done(g.iota(T.Hi[:], [[1, 128]], 0, 128), "Hi")
+    done(g.iota(T.W[:, 0:256], [[1, 256]], base, 0, allow_small_or_imprecise_dtypes=True), "W0")
     wait(g, "oneb")
     done(g.affine_select(T.Z0[:], T.oneb[:], [[32, 5], [1000, 2], [1, 16]], AluOpType.is_equal, 0.0, -1000, -1), "Z0")
     done(g.affine_select(T.Z1[:], T.oneb[:], [[32, 5], [1000, 2], [1, 16]], AluOpType.is_equal, 0.0, -16, -1), "Z1")
+    done(g.iota(T.pi[:, 0:1], [[1, 1]], 0, 1), "pi")
     done(g.iota(T.J96[:], [[1, M]], base + H, 0, allow_small_or_imprecise_dtypes=True), "J96")
-    done(g.dma_start(T.X2[:, 1536:H], T.x[:, 1536:H]), "ldX3", 16)
     wait(g, "onef")
     done(g.affine_select(T.Zp[:], T.onef[:], [[16, 10], [1001, 16]], AluOpType.is_equal, 0.0, -3016, -1), "Zp")
-    done(g.affine_select(T.Id[:], T.oneb[:, 0:128], [[-1, 128]], AluOpType.is_equal, 0.0, 0, 1), "Id")
     wait(g, "s0")
     exchange(0, T.s0, T.l0, 0, E)
+    done(g.affine_select(T.Id[:], T.oneb[:, 0:128], [[-1, 128]], AluOpType.is_equal, 0.0, 0, 1), "Id")
     wait(g, "s1")
     exchange(1, T.s1, T.l1, 0, E)
     wait(g, "Ca")
     done(g.dma_start(T.U[:, 0:1024], T.C[:, 0:1024], accum_op=add), "dUa", 16)
-    wait(g, "s2a", "s2c")
-    exchange(2, T.s2, T.l2, 0, 2 * E)
     wait(g, "Cb")
     done(g.dma_start(T.U[:, 1024:H], T.C[:, 1024:H], accum_op=add), "dUb", 16)
+    wait(g, "s2a", "s2c")
+    exchange(2, T.s2, T.l2, 0, 2 * E)
     wait(g, "s3")
     exchange(3, T.s3, T.Ds, H, E)
     wait(g, "q0", "q1", "q2")
@@ -158,6 +159,8 @@ def rank_program(g, core, T, topo):
     wait(P, "Ca", "Cb", "Id")
     for k, (a, b) in enumerate(quarter):
         P.matmul(T["PM%d" % k][:], T.Id[:], T.C[:, a:b], True, False)
+    wait(P, "Lp")
+    P.matmul(T.PL[:, 0:H - KV], T.Id[:], T.A[:, KV:H], True, False)
     wait(P, "s1", "s2a", "r2")
     P.matmul(T.PH[:, 0:M], T.Id[:], T.s1[:], True, False)
     P.matmul(T.PH[:, 0:M], T.Id[:], T.s2[:, 0:2 * M:2], False, False)
@@ -167,28 +170,32 @@ def rank_program(g, core, T, topo):
         done(P.matmul(T["PM%d" % k][:], T.Id[:], T.Ds[:, a:b], False, True), "PM%d" % k)
     wait(P, "Tt", "Ls")
     to_list(T.PG, 4, 5, "PT")
+    wait(P, "Un")
+    done(P.matmul(T.PL[:, 0:H - KV], T.Id[:], T.Un[:], False, True), "PK")
 
     done(S.dma_start(T.fari[:, 0:6], T.far[:]), "ldf", 16)
     wait(S, "W0")
-    for k in range(1, 4):
-        done(S.activation(T.W[:, 512 * k:512 * (k + 1)], T.W[:, 0:512], Copy), "Wc")
-    wait(S, "Wc", "HF")
-    done(S.dma_start(T.W[0::16, :], T.HF[:]), "ldH", 16)
-    done(S.dma_start(T.W[1::16, :], T.HF[:]), "ldH", 16)
-    wait(S, "ldH", "ldP", "FL", "mcol")
+    for k in range(4, 8):
+        done(S.activation(T.W[:, 256 * k:256 * (k + 1)], T.W[:, 0:256], Ident, bias=float(256 * k)), "Wc")
+    done(S.dma_start(T.X2[:, 0:512], T.x[:, 0:512]), "ldX0", 16)
+    wait(S, "ldP", "FL", "mcol")
     done(S.activation(T.s0[:], T.W[:].indirect(far), Ident, scale=T.mcol[:, 0:1]), "s0")
     wait(S, "Ltn")
     done(S.activation(T.SR[:], T.W[:].indirect(lst(Lt)), Copy), "SR")
     wait(S, *allA)
     for k, (a, b) in enumerate(third):
         done(S.activation(T.At[:, a:b], T.A[:].indirect(lst(Lt, a, b)), Copy), "At%d" % k)
+    wait(S, "At2")
+    done(S.activation(T.At2[:, third[2][0]:H], T.At[:, third[2][0]:H], Copy), "Atc")
+    wait(S, "SR2")
+    done(S.activation(T.TR[:, 0:384], T.SR[:].indirect(lst(Ln, 0, 384)), Copy), "TR")
     wait(S, "Ca", "Cb")
     done(S.activation(T.s2[:, 1:2 * M:2], T.C[:].indirect(far), Copy), "s2c")
-    wait(S, "SR2")
-    done(S.activation(T.TR[:], T.SR[:].indirect(lst(Ln)), Copy), "TR")
+    done(S.activation(T.TR[:, 384:H], T.SR[:].indirect(lst(Ln, 384, H)), Copy), "TR")
 
     def nxop(k, src, c):
         done(S.activation(T.NX[:, k:1024:8], src, Ident, bias=float(c), scale=8.0), "NX")
+    wait(S, "Fn")
     nxop(0, T.F[:, 0:128], 0)
     nxop(1, T.F[:, 0:128], 7)
     nxop(3, T.F[:, 128:256], 1)
@@ -196,44 +203,46 @@ def rank_program(g, core, T, topo):
     wait(S, "dSg")
     nxop(4, T.MS[:, 128:256], 4)
     nxop(5, T.MS[:, 128:256], 3)
+    wait(S, "dUa", "dUb")
+    done(S.activation(T.Un[:], T.U[:].indirect(lst(Ln, KV, H)), Copy), "Un")
+    wait(S, "dTg")
+    nxop(2, T.MS[:, 384:512], 6)
+    nxop(7, T.MS[:, 384:512], 5)
     wait(S, "PH")
     done(S.activation(T.M3[:, H:H + M], T.PH[:, 0:M], Copy), "M3")
     for k, (a, b) in enumerate(quarter):
         wait(S, "PM%d" % k)
         done(S.activation(T.M3[:, a:b], T["PM%d" % k][:], Copy), "M3")
-    wait(S, "dTg")
-    nxop(2, T.MS[:, 384:512], 6)
-    nxop(7, T.MS[:, 384:512], 5)
-    wait(S, "K")
-    a = 0
-    for k, w in enumerate(CHUNKS):
-        b = a + w
-        done(S.activation(T.Y[:, 4 * a:4 * b:4], T.K[:].indirect(lst(Ln, a, b)), Copy), "ys%d" % k)
-        if k == 0:
-            wait(S, "M3", "Lu")
+    wait(S, "PK")
+    done(S.activation(T.K[:, KV:H], T.PL[:, 0:H - KV], Copy), "Ke")
+    wait(S, "M3", "Lu")
+    for k in range(len(CHUNKS)):
+        a, b = edges[k], edges[k + 1]
         done(S.activation(T.Y[:, 4 * a + 1:4 * b:4], T.M3[:].indirect(lst(Lu, a, b)), Copy), "ys%d" % k)
-        a = b
+        if k == 0:
+            wait(S, "K", "Ke")
+        done(S.activation(T.Y[:, 4 * a:4 * b:4], T.K[:].indirect(lst(Ln, a, b)), Copy), "ys%d" % k)
 
     done(V.memset(T.oneb[:], 1.0), "oneb")
-    done(V.memset(T.W[:, 0:512], 0.0), "W0")
     done(V.memset(T.onef[:], 1.0), "onef")
     done(V.memset(T.At[:, H:H + M], 0.0), "Ath")
-    wait(V, "Hi")
-    done(V.tensor_scalar(T.Hj[:], T.Hi[:], H - 1, None, AluOpType.bitwise_and), "Hj")
-    done(V.tensor_scalar(T.mi[:, 0:1], T.Hi[:, 0:1], 7, 1, AluOpType.logical_shift_right, AluOpType.bitwise_and), "mi")
-    wait(V, "Hj")
-    done(V.tensor_scalar(T.HF[:], T.Hj[:], float(base), None, add), "HF")
-    wait(V, "mi")
-    done(V.tensor_copy(T.mcol[:, 0:1], T.mi[:, 0:1]), "mcol")
-    done(V.tensor_scalar(T.ncol[:, 0:1], T.mi[:, 0:1], -1.0, 1.0, mul, add), "ncol")
+    wait(V, "W0")
+    for k in range(1, 4):
+        done(V.tensor_scalar(T.W[:, 256 * k:256 * (k + 1)], T.W[:, 0:256], float(256 * k), None, add), "W1")
+    wait(V, "ldp")
+    done(V.tensor_copy(T.F[:, 128:256], T.Mi[:, 256:384]), "F")
     wait(V, "ldM")
-    done(V.tensor_copy(T.F[:], T.Mi[:, 128:384]), "F")
     done(V.tensor_scalar(T.h16[:, 0:384], T.Mi[:], float(base), float(H - 1), sub, mn), "h0")
     wait(V, "h0")
     for k in range(3):
         done(V.transpose(T.T16[:, k, :], T.h16[:, 128 * k:128 * (k + 1)]), "T0")
-    wait(V, "ldf")
+    wait(V, "ldf", "pi")
+    done(V.tensor_scalar(T.mi[:, 0:1], T.pi[:, 0:1], 1, None, AluOpType.bitwise_and), "mi")
     done(V.tensor_copy(far, T.fari[:, 0:6]), "FL")
+    wait(V, "mi")
+    done(V.tensor_copy(T.mcol[:, 0:1], T.mi[:, 0:1]), "mcol")
+    done(V.tensor_scalar(T.ncol[:, 0:1], T.mi[:, 0:1], -1.0, 1.0, mul, add), "ncol")
+    done(V.tensor_copy(T.F[:, 0:128], T.Mi[:, 128:256]), "Fn")
     wait(V, "J96", "ncol")
     done(V.tensor_scalar(T.K96[:], T.J96[:], T.ncol[:, 0:1], None, mul), "K96")
     wait(V, "PL")
@@ -244,21 +253,21 @@ def rank_program(g, core, T, topo):
         done(V.tensor_tensor(T.A[:, a:b], T.X[:].indirect(lst(Ln, a, b)), T.X2[:, a:b], add), "A%d" % k)
     wait(V, "FL", *allA)
     done(V.tensor_copy(T.s1[:], T.A[:].indirect(far)), "s1")
+    done(V.tensor_copy(T.L[:, Lp:Lp + 128], T.PL[:, 256:384]), "Lp")
     wait(V, "SR", "K96")
     done(V.tensor_copy(T.SR[:].indirect(far), T.K96[:]), "SR1")
     for k, (a, b) in enumerate(quarter):
+        if k == 3:
+            wait(V, "dSl")
+            done(V.tensor_scalar(T.h16[:, 384:512], T.MS[:, 0:128], float(base + 1024), None, sub), "hs")
+            wait(V, "hs")
+            done(V.transpose(T.T16[:, 3, :], T.h16[:, 384:512]), "Ts")
+            wait(V, "r0", "SR1")
+            done(V.tensor_tensor(T.SR[:].indirect(far), T.l0[:], T.K96[:], mx), "SR2")
         wait(V, "dA%d" % k)
         done(V.tensor_tensor(T.C[:, a:b], T.A[:].indirect(lst(Ln, a, b)), T.U[:, a:b], add), "Ca" if k < 2 else "Cb")
-    wait(V, "dSl")
-    done(V.tensor_scalar(T.h16[:, 384:512], T.MS[:, 0:128], float(base + 1024), None, sub), "hs")
-    wait(V, "hs")
-    done(V.transpose(T.T16[:, 3, :], T.h16[:, 384:512]), "Ts")
     wait(V, "PF")
     done(V.tensor_scalar(pf, T.PF[:, 0:6], float(base), None, sub), "PFL")
-    wait(V, "r0", "SR1")
-    done(V.tensor_tensor(T.SR[:].indirect(far), T.l0[:], T.K96[:], mx), "SR2")
-    wait(V, "At2")
-    done(V.tensor_copy(T.At2[:, third[2][0]:H], T.At[:, third[2][0]:H]), "Atc")
     wait(V, "r1", "dAt", "Atc")
     done(V.tensor_copy(T.At[:, 0:H].indirect(far), T.l1[:]), "Atp")
     wait(V, "Atp", "PFL")
@@ -267,28 +276,27 @@ def rank_program(g, core, T, topo):
     done(V.tensor_scalar(T.L[:, Ls:Ls + 128], T.PG[:, 0:128], 1024.0, None, add), "Ls")
     wait(V, "Ls", "Ath")
     done(V.tensor_tensor(T.Ds[:, 0:H], T.At[:].indirect(lst(Ls)), T.At2[:], add), "Ds")
-    done(V.tensor_copy(T.L[:, Lp:Lp + 128], T.PL[:, 256:384]), "Lp")
     wait(V, "Ds", "r2")
     done(V.tensor_tensor(T.Ds[:, 0:H].indirect(far), T.l1[:], T.l2[:, 0:2 * M:2], add), "Dsp")
     wait(V, "Dsp")
     done(V.tensor_copy(T.s3[:], T.Ds[:, 0:H].indirect(pf)), "s3")
-    wait(V, "dUa", "dUb")
-    done(V.tensor_tensor(T.K[:, 0:1024], T.U[:].indirect(lst(Ln, 0, 1024)), T.A[:, 0:1024], add), "K")
     wait(V, "dTl")
     done(V.tensor_scalar(T.h16[:, 512:640], T.MS[:, 256:384], float(base + 1024), None, sub), "ht")
     wait(V, "ht")
     done(V.transpose(T.T16[:, 4, :], T.h16[:, 512:640]), "Tt")
-    done(V.tensor_tensor(T.K[:, 1024:H], T.U[:].indirect(lst(Ln, 1024, H)), T.A[:, 1024:H], add), "K")
+    wait(V, "dUa", "dUb")
+    done(V.tensor_tensor(T.K[:, 0:KV], T.U[:].indirect(lst(Ln, 0, KV)), T.A[:, 0:KV], add), "K")
     wait(V, "PT")
     done(V.tensor_scalar(T.L[:, Lu:Lu + 128], T.PG[:, 0:128], 1024.0, None, add), "Lu")
     wait(V, "Lp")
-    a = 0
-    for k, w in enumerate(CHUNKS):
-        b = a + w
-        done(V.tensor_tensor(T.Y[:, 4 * a + 3:4 * b:4], T.At[:, 0:H].indirect(lst(Lp, a, b)), T.U[:, a:b], add), "yv%d" % k)
-        if a == 0:
-            wait(V, "r3", "dDa")
-        if a == 1024:
-            wait(V, "dDb")
-        done(V.tensor_tensor(T.Y[:, 4 * a + 2:4 * b:4], T.Ds[:].indirect(lst(Ls, a, b)), T.Ds2[:, a:b], add), "yv%d" % k)
-        a = b
+    for k in range(len(CHUNKS) + LEAD):
+        if k < len(CHUNKS):
+            a, b = edges[k], edges[k + 1]
+            done(V.tensor_tensor(T.Y[:, 4 * a + 3:4 * b:4], T.At[:, 0:H].indirect(lst(Lp, a, b)), T.U[:, a:b], add), "yv%d" % k)
+        if k >= LEAD:
+            a, b = edges[k - LEAD], edges[k - LEAD + 1]
+            if a == 0:
+                wait(V, "r3", "dDa")
+            if a <= 1024 < b:
+                wait(V, "dDb")
+            done(V.tensor_tensor(T.Y[:, 4 * a + 2:4 * b:4], T.Ds[:].indirect(lst(Ls, a, b)), T.Ds2[:, a:b], add), "yv%d" % (k - LEAD))

@@ -3,30 +3,42 @@ from concourse.mybir import AluOpType, ActivationFunctionType
 
 H, E, N = 2048, 32, 4
 M = (N - 1) * E
-CHUNKS = [256, 512, 512, 384, 256, 128]
-KV = 1536
-LEAD = 1
+CHUNKS = [224, 352, 416, 448, 384, 224]
+AX = [0, 384, 1152, H]
+AN = [0, 256, 768, 1408, H]
+GP = [0, 768, 1408, H]
+CH = 1152
+CC = [0, 768, H]
+YA = [1, 3, 5]
+V_ORDER = "A0 A1 g1 A2 s1 SR1 PFL g2 F0 F1 TSL hs Ts s2a F2 F3 Fq Ls G0 s3 SR2 v30 G1 hh Th G2 LU Gq v10 v35 v11 v00 v01 v12 v02 v13 v03 v04 v15 v05"
+S_ORDER = "s2n TR0 TR1 p1 p2 eU0 eU1 Ch p3 p4 eU2 eU3 nxu nxs s20 s21 u4 s22 s23 e14 s24 s25"
+G_ORDER = "J Zl Id ex0 ex1 aC0 ex2 aC1 ex3 aY0 aY1 c1 c2 c3 c4"
+Q_ORDER = "cC0 dSl dN cC1 cF0 cF1 dH dTg dSg nx o0 o1 o2 o3 o4 o5"
+P_ORDER = "PF PT PS mU0 mU1 mU2 mU3 PH PU m14"
 
-SB = {"bfloat16": {"X": H, "X2": H, "A": H, "U": H, "At": H + M, "At2": H, "C": H, "K": H, "Un": H - KV, "Ds": H + M, "Ds2": H,
-                   "M3": H + M, "Y": 4 * H, "oneb": 160, "Z0": 160, "Z1": 160, "Id": 128,
-                   "s1": M, "l1": M, "s2": 2 * M, "l2": 2 * M, "s3": M},
-      "float32": {"W": H, "SR": H, "TR": H, "F": 256, "MS": 512, "NX": 1024, "mcol": 4, "ncol": 4, "J96": M, "K96": M,
-                  "onef": 160, "Zp": 160, "s0": M, "l0": M},
-      "int32": {"Mi": 384, "pi": 4, "fari": 8, "mi": 4},
-      "uint16": {"L": 640, "FL": 8, "PFL": 8},
-      "float16": {"h16": 640}}
+SB = {"bfloat16": {"X": H, "X2": H, "A": H + M, "An": H, "C": H + 2 * M, "U": H, "F": H + M, "F2": H, "G": H + M,
+                   "Y3": H, "Cu": H, "Y": 4 * H, "oneb": 448, "Z0": 160, "Z1": 160, "Zl": 320,
+                   "Id": 256, "s1": M, "s2": 2 * M, "l2": 2 * M, "s3": M},
+      "float32": {"W": H, "SR": H, "TR": H, "NP": 512, "MS": 256, "MH": 256, "NX": 1024,
+                  "J": M, "D": M, "s0": M, "l0": M},
+      "int32": {"Mi": 384, "fari": 8},
+      "uint16": {"L": 768, "FL": 8, "PFL": 8, "TSL": 16},
+      "float16": {"h16": 768, "g1": M, "g2": M}}
 SCRATCH = {nm: ("sbuf", [128, w], d) for d in SB for nm, w in SB[d].items()}
-SCRATCH["T16"] = ("sbuf", [128, 5, 128], "float16")
+SCRATCH["T16"] = ("sbuf", [128, 6, 128], "float16")
 for _nm in ("PL", "PF", "PG", "PH", "PM0", "PM1", "PM2", "PM3"):
     SCRATCH[_nm] = ("psum", [128, 512], "float32")
-SEMAPHORES = (["ldM", "ldp", "ldx", "ldf", "ldP", "dSl", "dSg", "dTl", "dTg", "dUa", "dUb", "dDa", "dDb", "dAt", "out",
-               "r0", "r1", "r2", "r3", "q0", "q1", "q2", "q3",
-               "oneb", "onef", "W0", "W1", "Ath", "pi", "mi", "mcol", "ncol", "J96", "K96", "Z0", "Z1", "Zp", "Id",
-               "Wc", "F", "Fn", "h0", "T0", "FL", "PL", "Ltn", "Lp", "s0", "s1", "SR", "SR1", "SR2", "Ca", "Cb", "hs", "Ts", "PF",
-               "PFL", "At0", "At1", "At2", "Atc", "Atp", "s2a", "s2c", "PS", "Ls", "Ds", "Dsp", "s3", "K", "ht", "Tt", "PT",
-               "Lu", "TR", "NX", "PH", "PM0", "PM1", "PM2", "PM3", "M3", "Un", "PK", "Ke"]
-              + [nm + str(k) for nm in ("ldX", "A", "dA") for k in range(4)]
-              + ["yv%d" % k for k in range(len(CHUNKS))] + ["ys%d" % k for k in range(len(CHUNKS))])
+DMAS = ["ldp", "ldx", "ldf", "ldP", "ldX0", "ldX1", "ldX2", "dSl", "dSg", "dTg"]
+DMAS += [nm for nm in (G_ORDER + " " + Q_ORDER).split() if nm[:2] in ("aC", "aU", "aY", "cC", "cF", "ld")]
+SEMAPHORES = (DMAS + ["ldM", "dN", "dH", "out", "r0", "r1", "r2", "r3", "q0", "q1", "q2", "q3",
+                      "oneb", "two", "g1", "W0", "W1", "Fh", "J", "D", "Z0", "Z1", "Zl",
+                      "Id", "Wc", "Fp", "Fn", "h0", "T0", "FL", "PL", "Ltn", "s0", "s1", "g2", "SR", "SR1", "SR2",
+                      "hs", "Ts", "PF", "PFL", "PT", "TSL", "s2a", "s2n", "PS", "Ls", "Fq", "Fl", "s3", "Gq",
+                      "TR", "hh", "Th", "PU", "LU", "NX", "PH", "Ch"]
+              + [nm + str(k) for nm in ("A", "G", "mU", "yU") for k in range(4)]
+              + [nm + str(k) for nm in ("An", "F") for k in range(len(AN) - 1)]
+              + [nm for nm in S_ORDER.split() if nm[0] in "pu"] + [nm for nm in P_ORDER.split() if nm[:2] in ("m1", "m3")]
+              + [nm + str(k) for nm in ("y0", "y1", "y2", "y3") for k in range(len(CHUNKS))])
 
 
 def rank_program(g, core, T, topo):
@@ -34,28 +46,41 @@ def rank_program(g, core, T, topo):
     if rank is None:
         return
     V, S, P, Q = g.vector, g.scalar, g.tensor, g.sync
-    add, sub, mul, mx, mn = AluOpType.add, AluOpType.subtract, AluOpType.mult, AluOpType.max, AluOpType.min
+    add, sub, mn = AluOpType.add, AluOpType.subtract, AluOpType.min
     Copy, Ident = ActivationFunctionType.Copy, ActivationFunctionType.Identity
     base = H * rank
-    total = {"ldM": 32, "ldp": 16, "ldx": 16, "ldf": 16, "ldP": 32, "dSl": 16, "dSg": 16, "dTl": 16, "dTg": 16,
-             "dUa": 16, "dUb": 16, "dDa": 16, "dDb": 16, "dAt": 32, "out": 16 * (len(CHUNKS) + 1),
-             "Wc": 4, "W1": 3, "T0": 3, "NX": 8, "M3": 5, "Ca": 2, "Cb": 2, "TR": 2}
-    for k in range(len(CHUNKS)):
-        total["yv%d" % k] = 2
-        total["ys%d" % k] = 2
+    mid = base + 1024
+    total = {"ldM": 32, "dN": 32, "dH": 32, "out": 16 * (len(CHUNKS) + 1), "Wc": 4, "W1": 3, "NX": 8, "TR": 2, "D": 3}
+    for nm in DMAS:
+        total[nm] = 16
     for k in range(4):
         total["r%d" % k] = 2 * (N - 1)
         total["q%d" % k] = 2 * (N - 1)
-        for nm in ("ldX", "dA"):
-            total[nm + str(k)] = 16
-    allA = ["A%d" % k for k in range(4)]
+    allA = ["A%d" % k for k in range(len(AX) - 1)]
+    allG = ["G%d" % k for k in range(len(GP) - 1)]
+    allAn = ["An%d" % k for k in range(len(AN) - 1)]
+    allF = ["F%d" % k for k in range(len(AN) - 1)]
+    allC = ["aC%d" % k for k in range(len(CC) - 1)]
+    allY = ["aY%d" % k for k in range(len(YA) - 1)]
+    allU = [nm for nm in G_ORDER.split() if nm[:2] == "aU"]
+    Ub = T.A if allU else T.U
+    allU = allU or ["yU%d" % k for k in range(4)]
+    late = "cF2" in Q_ORDER.split()
+    warm = "ldT" in G_ORDER.split()
     quarter = [(512 * k, 512 * (k + 1)) for k in range(4)]
-    third = [(0, 768), (768, 1536), (1536, H)]
     edges = [sum(CHUNKS[:k]) for k in range(len(CHUNKS) + 1)]
+    pieces = [(edges[k], edges[k + 1]) for k in range(len(CHUNKS))]
+    sums = [nm for nm in P_ORDER.split() if nm[0] == "m"]
+    waited = []
+
+    def cover(names, cuts, a, b):
+        return [nm for k, nm in enumerate(names) if cuts[k] < b and cuts[k + 1] > a]
 
     def wait(q, *names):
         for nm in names:
-            q.wait_ge(T.sem[nm], total.get(nm, 1))
+            if not any(q is q2 and nm == nm2 for q2, nm2 in waited):
+                waited.append((q, nm))
+                q.wait_ge(T.sem[nm], total.get(nm, 1))
 
     def done(ins, nm, n=1):
         ins.then_inc(T.sem[nm], n)
@@ -72,231 +97,343 @@ def rank_program(g, core, T, topo):
                                          dst=dst[:, off + w * j:off + w * (j + 1)]))
         g.remote_dma_fused(trs, local_sem=T.sem["q%d" % k])
 
-    Lt, Ln, Lp, Ls, Lu = 0, 128, 256, 384, 512
-    far, pf = T.FL[:, 0:6], T.PFL[:, 0:6]
+    Lt, Ln, Lp, Ls, Lu, Lnn = 0, 128, 256, 384, 512, 640
+    far, pf, tpf, spf = T.FL[:, 0:6], T.PFL[:, 0:6], T.TSL[:, 0:6], T.TSL[:, 6:12]
 
     def lst(c0, a=0, b=H):
         return T.L[:, c0 + a // 16:c0 + b // 16]
 
-    def to_list(ps, t0, t1, ev):
-        nt = t1 - t0
+    def ylane(c, a, b):
+        return T.Y[:, 4 * a + c:4 * b:4]
+
+    def span(nm):
+        return (quarter if nm[1] == "U" else pieces)[int(nm[-1])]
+
+    def bank(nm):
+        a, b = span(nm)
+        return T["PM%d" % (sums.index(nm) % 4)][:, 0:b - a]
+
+    def q_step(nm):
+        if nm[0] == "o":
+            a, b = span(nm)
+            wait(Q, *["y%d%s" % (c, nm[1]) for c in range(4)])
+            done(Q.dma_start(T.y[:, 4 * a:4 * b], T.Y[:, 4 * a:4 * b]), "out", 16)
+            return
+        f2 = GP[2] if late else H
+        need, moves = {
+            "cC0": (cover(allA, AX, 0, CH), [(T.C[:, 0:CH], T.A[:, 0:CH])]),
+            "cC1": (allA, [(T.C[:, CH:H], T.A[:, CH:H])]),
+            "dSl": (["SR1"], [(T.NP[:, 384:512], T.SR[2::16, :])]),
+            "dN": (["g2", "Fn"] + ["ldT"] * warm, [(T.SR[4::16, :], T.NP[:, 128:256]), (T.SR[1::16, :], T.NP[:, 0:128])]),
+            "cF0": (["Fq"] if late else cover(allF, AN, 0, GP[1]), [(T.F2[:, 0:GP[1]], T.F[:, 0:GP[1]])]),
+            "cF1": (["Fq"], [(T.F2[:, GP[1]:f2], T.F[:, GP[1]:f2])]),
+            "cF2": (["Fq"], [(T.F2[:, GP[2]:H], T.F[:, GP[2]:H])]),
+            "dH": (["TR"], [(T.MH[:, 0:128], T.TR[0::16, :]), (T.MH[:, 128:256], T.TR[4::16, :])]),
+            "dTg": (["TR"], [(T.MS[:, 128:256], T.TR[1::16, :])]),
+            "dSg": (["SR2"], [(T.MS[:, 0:128], T.SR[2::16, :])]),
+            "nx": (["NX"], [(T.nx[:], T.NX[:])])}[nm]
+        wait(Q, *need)
+        for out, in_ in moves:
+            done(Q.dma_start(out, in_), "out" if nm == "nx" else nm, 16)
+
+    done(Q.dma_start(T.Mi[:, 0:128], T.twn[:]), "ldM", 16)
+    done(Q.dma_start(T.Mi[:, 128:256], T.nxt[:]), "ldM", 16)
+    done(Q.dma_start(T.X[:], T.x[:]), "ldx", 16)
+    done(Q.dma_start(T.X2[:, 0:AX[1]], T.x[:, 0:AX[1]]), "ldX0", 16)
+    wait(Q, "W0", "W1", "Wc", "Fp")
+    done(Q.dma_start(T.W[2::16, :], T.NP[:, 256:384]), "ldP", 16)
+    for k in range(1, len(allA)):
+        done(Q.dma_start(T.X2[:, AX[k]:AX[k + 1]], T.x[:, AX[k]:AX[k + 1]]), "ldX%d" % k, 16)
+    for nm in Q_ORDER.split():
+        q_step(nm)
+    wait(Q, "out")
+
+    def g_copy(out, in_, n, nm):
+        done(g.affine_select(out, in_, [[0, n]], AluOpType.is_equal, 0.0, 0, 0), nm)
+
+    def g_add(out, in_, nm):
+        done(g.dma_start(out, in_, accum_op=add), nm, 16)
+
+    def g_step(nm):
+        if nm == "J":
+            done(g.iota(T.J[:], [[1, M]], 1024, 0, allow_small_or_imprecise_dtypes=True), nm)
+        elif nm == "Zl":
+            done(g.affine_select(T.Zl[:], T.oneb[:, 0:320], [[-2000, 2], [16, 10], [1001, 16]], AluOpType.is_equal, 0.0, -16, -1), nm)
+        elif nm == "Id":
+            wait(g, "two")
+            done(g.affine_select(T.Id[:], T.oneb[:, 192:448], [[0, 2], [-1, 128]], AluOpType.is_equal, 0.0, 0, 1), nm)
+        elif nm == "ldT":
+            done(g.dma_start(T.NP[:, 0:128], T.twn[:]), nm, 16)
+        elif nm == "ex0":
+            wait(g, "s0")
+            exchange(0, T.s0, T.l0, 0, E)
+        elif nm == "ex1":
+            wait(g, "s1")
+            exchange(1, T.s1, T.A, H, E)
+        elif nm == "ex2":
+            wait(g, "s2a", "s2n")
+            exchange(2, T.s2, T.l2, 0, 2 * E)
+        elif nm == "ex3":
+            wait(g, "s3")
+            exchange(3, T.s3, T.G, H, E)
+        elif nm == "g1":
+            wait(g, "s0")
+            g_copy(T.g1[:], T.s0[:], M, nm)
+        elif nm == "hs":
+            wait(g, "dSl", "Fp")
+            g_copy(T.h16[:, 256:512], T.NP[:, 256:512], 256, nm)
+        elif nm == "hh":
+            wait(g, "dH")
+            g_copy(T.h16[:, 512:768], T.MH[:], 256, nm)
+        elif nm[:2] == "aC":
+            a, b = CC[int(nm[2])], CC[int(nm[2]) + 1]
+            wait(g, *(cover(["cC0", "cC1"], [0, CH, H], a, b) + cover(allAn, AN, a, b)))
+            g_add(T.C[:, a:b], T.An[:, a:b], nm)
+        elif nm[:2] == "aU":
+            a, b = (0, H) if nm == "aU" else (CC[int(nm[2])], CC[int(nm[2]) + 1])
+            wait(g, "s2a", "cC0", "cC1", *(cover(allC, CC, a, b) + allF))
+            g_add(T.A[:, a:b], T.C[:, a:b], nm)
+        elif nm[:2] == "aY":
+            k0, k1 = YA[int(nm[2])], YA[int(nm[2]) + 1]
+            a, b = edges[k0], edges[k1]
+            wait(g, *(["p%d" % k for k in range(k0, k1)] + cover(allC, CC, a, b)))
+            g_add(T.Y3[:, a:b], T.C[:, a:b], nm)
+        else:
+            k = int(nm[1])
+            a, b = pieces[k]
+            wait(g, *cover(allY, YA, k, k + 1))
+            g_copy(ylane(3, a, b), T.Y3[:, a:b], b - a, "y3%d" % k)
+
+    done(g.iota(T.W[:, 0:256], [[1, 256]], -1024, 0, allow_small_or_imprecise_dtypes=True), "W0")
+    wait(g, "oneb")
+    done(g.affine_select(T.Z0[:], T.oneb[:, 0:160], [[32, 5], [1000, 2], [1, 16]], AluOpType.is_equal, 0.0, -1000, -1), "Z0")
+    done(g.affine_select(T.Z1[:], T.oneb[:, 0:160], [[32, 5], [1000, 2], [1, 16]], AluOpType.is_equal, 0.0, -16, -1), "Z1")
+    for nm in G_ORDER.split():
+        g_step(nm)
+    wait(g, "q0", "q1", "q2", "q3")
+
+    def to_list(ps, t0, ev):
         for s in range(8):
             b, u = s // 2, s % 2
             z = T.Z1 if u else T.Z0
             for g1 in range(2):
                 o = 16 - 16 * (g1 - u)
                 c = 32 * b + 16 * g1
-                rhs = T.T16[:, t0, c:c + 16] if nt == 1 else T.T16[:, t0:t1, c:c + 16]
-                ins = P.matmul(ps[:, s:128 * nt:8], z[:, o:o + 128], rhs, g1 == 0, g1 == 1)
+                ins = P.matmul(ps[:, s:256:8], z[:, o:o + 128], T.T16[:, t0:t0 + 2, c:c + 16], g1 == 0, g1 == 1)
         done(ins, ev)
 
-    done(Q.dma_start(T.Mi[:, 256:384], T.prv[:]), "ldp", 16)
-    done(Q.dma_start(T.Mi[:, 0:128], T.twn[:]), "ldM", 16)
-    done(Q.dma_start(T.Mi[:, 128:256], T.nxt[:]), "ldM", 16)
-    done(Q.dma_start(T.X[:], T.x[:]), "ldx", 16)
-    wait(Q, "W0", "W1", "Wc", "F")
-    done(Q.dma_start(T.W[2::16, :], T.F[:, 128:256]), "ldP", 16)
-    done(Q.dma_start(T.W[3::16, :], T.F[:, 128:256]), "ldP", 16)
-    for k in (1, 2, 3):
-        a, b = quarter[k]
-        done(Q.dma_start(T.X2[:, a:b], T.x[:, a:b]), "ldX%d" % k, 16)
-    for k, (a, b) in enumerate(quarter):
-        wait(Q, "A%d" % k)
-        done(Q.dma_start(T.U[:, a:b], T.A[:, a:b]), "dA%d" % k, 16)
-    wait(Q, "SR1")
-    done(Q.dma_start(T.MS[:, 0:128], T.SR[2::16, :]), "dSl", 16)
-    for k, (a, b) in enumerate(third[0:2]):
-        wait(Q, "At%d" % k)
-        done(Q.dma_start(T.At2[:, a:b], T.At[:, a:b]), "dAt", 16)
-    wait(Q, "SR2")
-    done(Q.dma_start(T.MS[:, 128:256], T.SR[3::16, :]), "dSg", 16)
-    wait(Q, "TR")
-    done(Q.dma_start(T.MS[:, 256:384], T.TR[0::16, :]), "dTl", 16)
-    done(Q.dma_start(T.MS[:, 384:512], T.TR[1::16, :]), "dTg", 16)
-    wait(Q, "Dsp")
-    done(Q.dma_start(T.Ds2[:, 0:1024], T.Ds[:, 0:1024]), "dDa", 16)
-    wait(Q, "q3")
-    done(Q.dma_start(T.Ds2[:, 1024:H], T.Ds[:, 1024:H]), "dDb", 16)
-    wait(Q, "NX")
-    done(Q.dma_start(T.nx[:], T.NX[:]), "out", 16)
-    for k in range(len(CHUNKS)):
-        a, b = edges[k], edges[k + 1]
-        wait(Q, "yv%d" % k, "ys%d" % k)
-        done(Q.dma_start(T.y[:, 4 * a:4 * b], T.Y[:, 4 * a:4 * b]), "out", 16)
-    wait(Q, "out")
+    def lane_to_list(ps, c0, lane, src):
+        for i in range(16):
+            ins = P.matmul(ps[:, c0:c0 + 6], T.Zl[:, 81 * lane + 16 - i:81 * lane + 144 - i], src[:, i:M:16], i == 0, i == 15)
+        return ins
 
-    done(g.iota(T.W[:, 0:256], [[1, 256]], base, 0, allow_small_or_imprecise_dtypes=True), "W0")
-    wait(g, "oneb")
-    done(g.affine_select(T.Z0[:], T.oneb[:], [[32, 5], [1000, 2], [1, 16]], AluOpType.is_equal, 0.0, -1000, -1), "Z0")
-    done(g.affine_select(T.Z1[:], T.oneb[:], [[32, 5], [1000, 2], [1, 16]], AluOpType.is_equal, 0.0, -16, -1), "Z1")
-    done(g.iota(T.pi[:, 0:1], [[1, 1]], 0, 1), "pi")
-    done(g.iota(T.J96[:], [[1, M]], base + H, 0, allow_small_or_imprecise_dtypes=True), "J96")
-    wait(g, "onef")
-    done(g.affine_select(T.Zp[:], T.onef[:], [[16, 10], [1001, 16]], AluOpType.is_equal, 0.0, -3016, -1), "Zp")
-    wait(g, "s0")
-    exchange(0, T.s0, T.l0, 0, E)
-    done(g.affine_select(T.Id[:], T.oneb[:, 0:128], [[-1, 128]], AluOpType.is_equal, 0.0, 0, 1), "Id")
-    wait(g, "s1")
-    exchange(1, T.s1, T.l1, 0, E)
-    wait(g, "Ca")
-    done(g.dma_start(T.U[:, 0:1024], T.C[:, 0:1024], accum_op=add), "dUa", 16)
-    wait(g, "Cb")
-    done(g.dma_start(T.U[:, 1024:H], T.C[:, 1024:H], accum_op=add), "dUb", 16)
-    wait(g, "s2a", "s2c")
-    exchange(2, T.s2, T.l2, 0, 2 * E)
-    wait(g, "s3")
-    exchange(3, T.s3, T.Ds, H, E)
-    wait(g, "q0", "q1", "q2")
+    def psum_add(ps, parts, twice=False):
+        for k, part in enumerate(parts):
+            c = 128 if twice and k == 0 else 0
+            ins = P.matmul(ps, T.Id[:, c:c + 128], part, k == 0, k == len(parts) - 1)
+        return ins
+
+    def p_step(nm):
+        if nm == "PF":
+            wait(P, "g1", "Zl")
+            done(lane_to_list(T.PF, 0, 2, T.g1), nm)
+        elif nm == "PT":
+            wait(P, "g2", "Zl")
+            lane_to_list(T.PH, 0, 0, T.g2)
+            done(lane_to_list(T.PH, 6, 2, T.g2), nm)
+        elif nm == "PS":
+            wait(P, "Ts")
+            to_list(T.PG, 2, nm)
+        elif nm == "PH":
+            wait(P, "Id", "r1", "r2", "s2n", "PFL")
+            psum_add(T.PF[:, 0:M], [T.A[:, H:H + M], T.l2[:, 1:2 * M:2]])
+            done(psum_add(T.PF[:, M:2 * M], [T.A[:, H:H + M], T.s2[:, 1:2 * M:2], T.l2[:, 0:2 * M:2]]), nm)
+        elif nm == "PU":
+            wait(P, "Th", "Ltn")
+            to_list(T.PL, 4, nm)
+        else:
+            a, b = span(nm)
+            j = sums.index(nm)
+            wait(P, "Id", *(["y" + sums[j - 4][1:]] if j >= 4 else []))
+            if nm[1] == "U":
+                wait(P, *cover(allAn, AN, a, b))
+                done(psum_add(bank(nm), [T.A[:, a:b], T.An[:, a:b]], True), nm)
+            elif nm[1] == "1":
+                wait(P, "Fq", "u" + nm[2])
+                done(psum_add(bank(nm), [T.F[:, a:b], T.Cu[:, a:b]]), nm)
+            else:
+                wait(P, "p" + nm[2], *cover(allC, CC, a, b))
+                done(psum_add(bank(nm), [T.C[:, a:b], T.Y3[:, a:b]]), nm)
 
     wait(P, "T0", "Z0", "Z1")
-    to_list(T.PL, 0, 3, "PL")
-    wait(P, "s0", "Zp")
-    for i in range(16):
-        ins = P.matmul(T.PF[:, 0:6], T.Zp[:, 19 - i:147 - i], T.s0[:, i:M:16], i == 0, i == 15)
-    done(ins, "PF")
-    wait(P, "Ts")
-    to_list(T.PG, 3, 4, "PS")
-    wait(P, "Ca", "Cb", "Id")
-    for k, (a, b) in enumerate(quarter):
-        P.matmul(T["PM%d" % k][:], T.Id[:], T.C[:, a:b], True, False)
-    wait(P, "Lp")
-    P.matmul(T.PL[:, 0:H - KV], T.Id[:], T.A[:, KV:H], True, False)
-    wait(P, "s1", "s2a", "r2")
-    P.matmul(T.PH[:, 0:M], T.Id[:], T.s1[:], True, False)
-    P.matmul(T.PH[:, 0:M], T.Id[:], T.s2[:, 0:2 * M:2], False, False)
-    done(P.matmul(T.PH[:, 0:M], T.Id[:], T.l2[:, 1:2 * M:2], False, True), "PH")
-    wait(P, "Dsp")
-    for k, (a, b) in enumerate(quarter):
-        done(P.matmul(T["PM%d" % k][:], T.Id[:], T.Ds[:, a:b], False, True), "PM%d" % k)
-    wait(P, "Tt", "Ls")
-    to_list(T.PG, 4, 5, "PT")
-    wait(P, "Un")
-    done(P.matmul(T.PL[:, 0:H - KV], T.Id[:], T.Un[:], False, True), "PK")
+    to_list(T.PL, 0, "PL")
+    for nm in P_ORDER.split():
+        p_step(nm)
 
+    def nxop(k, src, c):
+        done(S.activation(T.NX[:, k:1024:8], src, Ident, bias=float(c), scale=8.0), "NX")
+
+    def s_step(nm):
+        if nm == "s2n":
+            wait(S, *allAn)
+            done(S.activation(T.s2[:, 1:2 * M:2], T.An[:].indirect(far), Copy), nm)
+        elif nm in ("TR0", "TR1"):
+            a = 1024 * int(nm[2])
+            wait(S, "dN")
+            done(S.activation(T.TR[:, a:a + 1024], T.SR[:].indirect(lst(Ln, a, a + 1024)), Copy), "TR")
+        elif nm == "Ch":
+            wait(S, "PH")
+            done(S.activation(T.C[:, H:H + 2 * M], T.PF[:, 0:2 * M], Copy), nm)
+        elif nm == "nxu":
+            wait(S, "dTg")
+            nxop(2, T.MS[:, 128:256], 8 * mid * (1 - warm) + 6)
+            nxop(7, T.MS[:, 128:256], 8 * mid * (1 - warm) + 5)
+        elif nm == "nxs":
+            wait(S, "dSg")
+            nxop(4, T.MS[:, 0:128], 8 * mid + 4)
+            nxop(5, T.MS[:, 0:128], 8 * mid + 3)
+        else:
+            a, b = span(nm)
+            if nm[0] == "p":
+                wait(S, "Fq", "Ls")
+                done(S.activation(T.Y3[:, a:b], T.F[:, 0:H].indirect(lst(Lp, a, b)), Copy), nm)
+            elif nm[0] == "u":
+                wait(S, "Ch", "LU", *allC)
+                done(S.activation(T.Cu[:, a:b], T.C[:, 0:H + M].indirect(lst(Lu, a, b)), Copy), nm)
+            elif nm[0] == "e":
+                wait(S, "m" + nm[1:])
+                out = T.U[:, a:b] if nm[1] == "U" else ylane(int(nm[1]), a, b)
+                done(S.activation(out, bank("m" + nm[1:]), Copy), "y" + nm[1:])
+            else:
+                wait(S, "r3", "Ls", *(["Gq"] if "Gq" in V_ORDER.split() else allG))
+                done(S.activation(ylane(2, a, b), T.G[:].indirect(lst(Ls, a, b)), Copy), "y" + nm[1:])
+
+    done(S.dma_start(T.Mi[:, 256:384], T.prv[:]), "ldp", 16)
     done(S.dma_start(T.fari[:, 0:6], T.far[:]), "ldf", 16)
     wait(S, "W0")
     for k in range(4, 8):
         done(S.activation(T.W[:, 256 * k:256 * (k + 1)], T.W[:, 0:256], Ident, bias=float(256 * k)), "Wc")
-    done(S.dma_start(T.X2[:, 0:512], T.x[:, 0:512]), "ldX0", 16)
-    wait(S, "ldP", "FL", "mcol")
-    done(S.activation(T.s0[:], T.W[:].indirect(far), Ident, scale=T.mcol[:, 0:1]), "s0")
+    wait(S, "Fp", "oneb")
+    nxop(3, T.NP[:, 256:384], 8 * mid + 1)
+    nxop(6, T.NP[:, 256:384], 8 * mid + 2)
+    for i in range(N - 1):
+        done(S.activation(T.D[:, E * i:E * (i + 1)], T.oneb[:, 0:E], Copy, scale=float(H * (i + (i >= rank) - rank))), "D")
+    wait(S, "Fn")
+    nxop(0, T.NP[:, 128:256], 8 * mid)
+    nxop(1, T.NP[:, 128:256], 8 * mid + 7)
+    wait(S, "ldP", "FL")
+    done(S.activation(T.s0[:], T.W[:].indirect(far), Copy), "s0")
     wait(S, "Ltn")
     done(S.activation(T.SR[:], T.W[:].indirect(lst(Lt)), Copy), "SR")
     wait(S, *allA)
-    for k, (a, b) in enumerate(third):
-        done(S.activation(T.At[:, a:b], T.A[:].indirect(lst(Lt, a, b)), Copy), "At%d" % k)
-    wait(S, "At2")
-    done(S.activation(T.At2[:, third[2][0]:H], T.At[:, third[2][0]:H], Copy), "Atc")
-    wait(S, "SR2")
-    done(S.activation(T.TR[:, 0:384], T.SR[:].indirect(lst(Ln, 0, 384)), Copy), "TR")
-    wait(S, "Ca", "Cb")
-    done(S.activation(T.s2[:, 1:2 * M:2], T.C[:].indirect(far), Copy), "s2c")
-    done(S.activation(T.TR[:, 384:H], T.SR[:].indirect(lst(Ln, 384, H)), Copy), "TR")
+    for k, nm in enumerate(allAn):
+        a, b = AN[k], AN[k + 1]
+        done(S.activation(T.An[:, a:b], T.A[:, 0:H].indirect(lst(Ln, a, b)), Copy), nm)
+    for nm in S_ORDER.split():
+        s_step(nm)
 
-    def nxop(k, src, c):
-        done(S.activation(T.NX[:, k:1024:8], src, Ident, bias=float(c), scale=8.0), "NX")
-    wait(S, "Fn")
-    nxop(0, T.F[:, 0:128], 0)
-    nxop(1, T.F[:, 0:128], 7)
-    nxop(3, T.F[:, 128:256], 1)
-    nxop(6, T.F[:, 128:256], 2)
-    wait(S, "dSg")
-    nxop(4, T.MS[:, 128:256], 4)
-    nxop(5, T.MS[:, 128:256], 3)
-    wait(S, "dUa", "dUb")
-    done(S.activation(T.Un[:], T.U[:].indirect(lst(Ln, KV, H)), Copy), "Un")
-    wait(S, "dTg")
-    nxop(2, T.MS[:, 384:512], 6)
-    nxop(7, T.MS[:, 384:512], 5)
-    wait(S, "PH")
-    done(S.activation(T.M3[:, H:H + M], T.PH[:, 0:M], Copy), "M3")
-    for k, (a, b) in enumerate(quarter):
-        wait(S, "PM%d" % k)
-        done(S.activation(T.M3[:, a:b], T["PM%d" % k][:], Copy), "M3")
-    wait(S, "PK")
-    done(S.activation(T.K[:, KV:H], T.PL[:, 0:H - KV], Copy), "Ke")
-    wait(S, "M3", "Lu")
-    for k in range(len(CHUNKS)):
-        a, b = edges[k], edges[k + 1]
-        done(S.activation(T.Y[:, 4 * a + 1:4 * b:4], T.M3[:].indirect(lst(Lu, a, b)), Copy), "ys%d" % k)
-        if k == 0:
-            wait(S, "K", "Ke")
-        done(S.activation(T.Y[:, 4 * a:4 * b:4], T.K[:].indirect(lst(Ln, a, b)), Copy), "ys%d" % k)
+    seen = []
 
-    done(V.memset(T.oneb[:], 1.0), "oneb")
-    done(V.memset(T.onef[:], 1.0), "onef")
-    done(V.memset(T.At[:, H:H + M], 0.0), "Ath")
+    def v_step(nm):
+        if nm == "g1":
+            wait(V, "s0")
+            done(V.tensor_copy(T.g1[:], T.s0[:]), nm)
+        elif nm == "s1":
+            wait(V, "FL", *allA)
+            done(V.tensor_copy(T.s1[:], T.A[:, 0:H].indirect(far)), nm)
+        elif nm == "PFL":
+            wait(V, "PF")
+            done(V.tensor_scalar(pf, T.PF[:, 0:6], 1024.0, None, add), nm)
+        elif nm == "SR1":
+            wait(V, "SR", "J")
+            done(V.tensor_copy(T.SR[:].indirect(far), T.J[:]), nm)
+        elif nm == "g2":
+            wait(V, "SR1", "PFL")
+            done(V.tensor_copy(T.g2[:], T.SR[:].indirect(pf)), nm)
+        elif nm == "TSL":
+            wait(V, "PT")
+            done(V.tensor_scalar(T.TSL[:, 0:12], T.PH[:, 0:12], 1024.0, None, add), nm)
+        elif nm == "s2a":
+            wait(V, "r1", "TSL", "s1")
+            done(V.tensor_tensor(T.s2[:, 0:2 * M:2], T.A[:].indirect(tpf), T.s1[:], add), nm)
+        elif nm == "hs":
+            wait(V, "dSl", "Fp")
+            done(V.tensor_copy(T.h16[:, 256:512], T.NP[:, 256:512]), nm)
+        elif nm == "Ts":
+            wait(V, "hs")
+            done(V.transpose(T.T16[:, 2:4, :], T.h16[:, 256:512]), nm)
+        elif nm == "Ls":
+            wait(V, "PS")
+            done(V.tensor_scalar(T.L[:, Lp:Lp + 256], T.PG[:, 0:256], 1024.0, None, add), nm)
+        elif nm == "Fq":
+            wait(V, "r1", "s2n", *(allF + ([] if late else ["cF0"])))
+            done(V.tensor_tensor(T.F[:, 0:H].indirect(far), T.s2[:, 1:2 * M:2], T.A[:, H:H + M], add), nm)
+        elif nm == "s3":
+            wait(V, "r2", "Fh", *seen)
+            done(V.tensor_copy(T.F[:, H:H + M], T.l2[:, 0:2 * M:2]), "Fl")
+            wait(V, "Fl", "Fq", "s2a")
+            done(V.tensor_tensor(T.s3[:], T.F[:].indirect(spf), T.s2[:, 0:2 * M:2], add), nm)
+        elif nm == "hh":
+            wait(V, "dH")
+            done(V.tensor_copy(T.h16[:, 512:768], T.MH[:]), nm)
+        elif nm == "Th":
+            wait(V, "hh")
+            done(V.transpose(T.T16[:, 4:6, :], T.h16[:, 512:768]), nm)
+        elif nm == "SR2":
+            wait(V, "r0", "TR", "D", "dSl")
+            done(V.tensor_tensor(T.SR[:].indirect(far), T.l0[:], T.D[:], add), nm)
+        elif nm == "LU":
+            wait(V, "PU")
+            done(V.tensor_scalar(T.L[:, Lu:Lu + 256], T.PL[:, 0:256], 1024.0, None, add), nm)
+        elif nm == "Gq":
+            wait(V, "Ch", *allG)
+            done(V.tensor_copy(T.G[:, 0:H].indirect(far), T.C[:, H + M:H + 2 * M]), nm)
+        elif nm[0] == "A":
+            k = int(nm[1])
+            a, b = AX[k], AX[k + 1]
+            wait(V, "ldX%d" % k)
+            done(V.tensor_tensor(T.A[:, a:b], T.X[:].indirect(lst(Ln, a, b)), T.X2[:, a:b], add), nm)
+        elif nm[0] == "F":
+            k = int(nm[1])
+            a, b = AN[k], AN[k + 1]
+            wait(V, allAn[k])
+            done(V.tensor_tensor(T.F[:, a:b], T.A[:, 0:H].indirect(lst(Lt, a, b)), T.An[:, a:b], add), nm)
+        elif nm[0] == "G":
+            k = int(nm[1])
+            a, b = GP[k], GP[k + 1]
+            wait(V, "Fq", "Ls", "Fh", *(["cF%d" % min(k, 2)] if late else ["cF1"] if k else []))
+            done(V.tensor_tensor(T.G[:, a:b], T.F[:].indirect(lst(Ls, a, b)), T.F2[:, a:b], add), nm)
+            seen.append(nm)
+        else:
+            a, b = span(nm)
+            if nm[1] == "0":
+                wait(V, "LU", *allU)
+                win, c0, other = Ub[:, 0:H], Lnn, T.An
+            elif nm[1] == "1":
+                wait(V, "LU", "Ch", "Fq", *allC)
+                win, c0, other = T.C[:, 0:H + M], Lu, T.F
+            else:
+                wait(V, "Ls", "Fq", *cover(allC, CC, a, b))
+                win, c0, other = T.F[:, 0:H], Lp, T.C
+            done(V.tensor_tensor(ylane(int(nm[1]), a, b), win.indirect(lst(c0, a, b)), other[:, a:b], add), "y" + nm[1:])
+
+    done(V.memset(T.oneb[:, 0:320], 1.0), "oneb")
+    done(V.memset(T.F[:, H:H + M], 0.0), "Fh")
+    done(V.memset(T.oneb[:, 320:448], 2.0), "two")
     wait(V, "W0")
     for k in range(1, 4):
         done(V.tensor_scalar(T.W[:, 256 * k:256 * (k + 1)], T.W[:, 0:256], float(256 * k), None, add), "W1")
     wait(V, "ldp")
-    done(V.tensor_copy(T.F[:, 128:256], T.Mi[:, 256:384]), "F")
+    done(V.tensor_scalar(T.NP[:, 256:384], T.Mi[:, 256:384], float(mid), None, sub), "Fp")
     wait(V, "ldM")
-    done(V.tensor_scalar(T.h16[:, 0:384], T.Mi[:], float(base), float(H - 1), sub, mn), "h0")
+    done(V.tensor_scalar(T.h16[:, 0:256], T.Mi[:, 0:256], float(base), float(H - 1), sub, mn), "h0")
     wait(V, "h0")
-    for k in range(3):
-        done(V.transpose(T.T16[:, k, :], T.h16[:, 128 * k:128 * (k + 1)]), "T0")
-    wait(V, "ldf", "pi")
-    done(V.tensor_scalar(T.mi[:, 0:1], T.pi[:, 0:1], 1, None, AluOpType.bitwise_and), "mi")
+    done(V.transpose(T.T16[:, 0:2, :], T.h16[:, 0:256]), "T0")
+    wait(V, "ldf")
     done(V.tensor_copy(far, T.fari[:, 0:6]), "FL")
-    wait(V, "mi")
-    done(V.tensor_copy(T.mcol[:, 0:1], T.mi[:, 0:1]), "mcol")
-    done(V.tensor_scalar(T.ncol[:, 0:1], T.mi[:, 0:1], -1.0, 1.0, mul, add), "ncol")
-    done(V.tensor_copy(T.F[:, 0:128], T.Mi[:, 128:256]), "Fn")
-    wait(V, "J96", "ncol")
-    done(V.tensor_scalar(T.K96[:], T.J96[:], T.ncol[:, 0:1], None, mul), "K96")
+    done(V.tensor_scalar(T.NP[:, 128 * warm:256], T.Mi[:, 128 * warm:256], float(mid), None, sub), "Fn")
     wait(V, "PL")
     done(V.tensor_copy(T.L[:, 0:256], T.PL[:, 0:256]), "Ltn")
     wait(V, "Ltn", "ldx")
-    for k, (a, b) in enumerate(quarter):
-        wait(V, "ldX%d" % k)
-        done(V.tensor_tensor(T.A[:, a:b], T.X[:].indirect(lst(Ln, a, b)), T.X2[:, a:b], add), "A%d" % k)
-    wait(V, "FL", *allA)
-    done(V.tensor_copy(T.s1[:], T.A[:].indirect(far)), "s1")
-    done(V.tensor_copy(T.L[:, Lp:Lp + 128], T.PL[:, 256:384]), "Lp")
-    wait(V, "SR", "K96")
-    done(V.tensor_copy(T.SR[:].indirect(far), T.K96[:]), "SR1")
-    for k, (a, b) in enumerate(quarter):
-        if k == 3:
-            wait(V, "dSl")
-            done(V.tensor_scalar(T.h16[:, 384:512], T.MS[:, 0:128], float(base + 1024), None, sub), "hs")
-            wait(V, "hs")
-            done(V.transpose(T.T16[:, 3, :], T.h16[:, 384:512]), "Ts")
-            wait(V, "r0", "SR1")
-            done(V.tensor_tensor(T.SR[:].indirect(far), T.l0[:], T.K96[:], mx), "SR2")
-        wait(V, "dA%d" % k)
-        done(V.tensor_tensor(T.C[:, a:b], T.A[:].indirect(lst(Ln, a, b)), T.U[:, a:b], add), "Ca" if k < 2 else "Cb")
-    wait(V, "PF")
-    done(V.tensor_scalar(pf, T.PF[:, 0:6], float(base), None, sub), "PFL")
-    wait(V, "r1", "dAt", "Atc")
-    done(V.tensor_copy(T.At[:, 0:H].indirect(far), T.l1[:]), "Atp")
-    wait(V, "Atp", "PFL")
-    done(V.tensor_copy(T.s2[:, 0:2 * M:2], T.At[:, 0:H].indirect(pf)), "s2a")
-    wait(V, "PS")
-    done(V.tensor_scalar(T.L[:, Ls:Ls + 128], T.PG[:, 0:128], 1024.0, None, add), "Ls")
-    wait(V, "Ls", "Ath")
-    done(V.tensor_tensor(T.Ds[:, 0:H], T.At[:].indirect(lst(Ls)), T.At2[:], add), "Ds")
-    wait(V, "Ds", "r2")
-    done(V.tensor_tensor(T.Ds[:, 0:H].indirect(far), T.l1[:], T.l2[:, 0:2 * M:2], add), "Dsp")
-    wait(V, "Dsp")
-    done(V.tensor_copy(T.s3[:], T.Ds[:, 0:H].indirect(pf)), "s3")
-    wait(V, "dTl")
-    done(V.tensor_scalar(T.h16[:, 512:640], T.MS[:, 256:384], float(base + 1024), None, sub), "ht")
-    wait(V, "ht")
-    done(V.transpose(T.T16[:, 4, :], T.h16[:, 512:640]), "Tt")
-    wait(V, "dUa", "dUb")
-    done(V.tensor_tensor(T.K[:, 0:KV], T.U[:].indirect(lst(Ln, 0, KV)), T.A[:, 0:KV], add), "K")
-    wait(V, "PT")
-    done(V.tensor_scalar(T.L[:, Lu:Lu + 128], T.PG[:, 0:128], 1024.0, None, add), "Lu")
-    wait(V, "Lp")
-    for k in range(len(CHUNKS) + LEAD):
-        if k < len(CHUNKS):
-            a, b = edges[k], edges[k + 1]
-            done(V.tensor_tensor(T.Y[:, 4 * a + 3:4 * b:4], T.At[:, 0:H].indirect(lst(Lp, a, b)), T.U[:, a:b], add), "yv%d" % k)
-        if k >= LEAD:
-            a, b = edges[k - LEAD], edges[k - LEAD + 1]
-            if a == 0:
-                wait(V, "r3", "dDa")
-            if a <= 1024 < b:
-                wait(V, "dDb")
-            done(V.tensor_tensor(T.Y[:, 4 * a + 2:4 * b:4], T.Ds[:].indirect(lst(Ls, a, b)), T.Ds2[:, a:b], add), "yv%d" % (k - LEAD))
+    for nm in V_ORDER.split():
+        v_step(nm)

from concourse.bass import DstId, RemoteDMATransfer
from concourse.mybir import AluOpType, ActivationFunctionType

H, E, N = 2048, 32, 4
M = (N - 1) * E
CHUNKS = [224, 352, 416, 448, 384, 224]
AX = [0, 384, 1152, H]
AN = [0, 256, 768, 1408, H]
GP = [0, 768, 1408, H]
CH = 1152
CC = [0, 768, H]
YA = [1, 3, 5]
V_ORDER = "A0 A1 g1 A2 s1 SR1 PFL g2 F0 F1 TSL hs Ts s2a F2 F3 Fq Ls G0 s3 SR2 v30 G1 hh Th G2 LU Gq v10 v35 v11 v00 v01 v12 v02 v13 v03 v04 v15 v05"
S_ORDER = "s2n TR0 TR1 p1 p2 eU0 eU1 Ch p3 p4 eU2 eU3 nxu nxs s20 s21 u4 s22 s23 e14 s24 s25"
G_ORDER = "J Zl Id ex0 ex1 aC0 ex2 aC1 ex3 aY0 aY1 c1 c2 c3 c4"
Q_ORDER = "cC0 dSl dN cC1 cF0 cF1 dH dTg dSg nx o0 o1 o2 o3 o4 o5"
P_ORDER = "PF PT PS mU0 mU1 mU2 mU3 PH PU m14"

SB = {"bfloat16": {"X": H, "X2": H, "A": H + M, "An": H, "C": H + 2 * M, "U": H, "F": H + M, "F2": H, "G": H + M,
                   "Y3": H, "Cu": H, "Y": 4 * H, "oneb": 448, "Z0": 160, "Z1": 160, "Zl": 320,
                   "Id": 256, "s1": M, "s2": 2 * M, "l2": 2 * M, "s3": M},
      "float32": {"W": H, "SR": H, "TR": H, "NP": 512, "MS": 256, "MH": 256, "NX": 1024,
                  "J": M, "D": M, "s0": M, "l0": M},
      "int32": {"Mi": 384, "fari": 8},
      "uint16": {"L": 768, "FL": 8, "PFL": 8, "TSL": 16},
      "float16": {"h16": 768, "g1": M, "g2": M}}
SCRATCH = {nm: ("sbuf", [128, w], d) for d in SB for nm, w in SB[d].items()}
SCRATCH["T16"] = ("sbuf", [128, 6, 128], "float16")
for _nm in ("PL", "PF", "PG", "PH", "PM0", "PM1", "PM2", "PM3"):
    SCRATCH[_nm] = ("psum", [128, 512], "float32")
DMAS = ["ldp", "ldx", "ldf", "ldP", "ldX0", "ldX1", "ldX2", "dSl", "dSg", "dTg"]
DMAS += [nm for nm in (G_ORDER + " " + Q_ORDER).split() if nm[:2] in ("aC", "aU", "aY", "cC", "cF", "ld")]
SEMAPHORES = (DMAS + ["ldM", "dN", "dH", "out", "r0", "r1", "r2", "r3", "q0", "q1", "q2", "q3",
                      "oneb", "two", "g1", "W0", "W1", "Fh", "J", "D", "Z0", "Z1", "Zl",
                      "Id", "Wc", "Fp", "Fn", "h0", "T0", "FL", "PL", "Ltn", "s0", "s1", "g2", "SR", "SR1", "SR2",
                      "hs", "Ts", "PF", "PFL", "PT", "TSL", "s2a", "s2n", "PS", "Ls", "Fq", "Fl", "s3", "Gq",
                      "TR", "hh", "Th", "PU", "LU", "NX", "PH", "Ch"]
              + [nm + str(k) for nm in ("A", "G", "mU", "yU") for k in range(4)]
              + [nm + str(k) for nm in ("An", "F") for k in range(len(AN) - 1)]
              + [nm for nm in S_ORDER.split() if nm[0] in "pu"] + [nm for nm in P_ORDER.split() if nm[:2] in ("m1", "m3")]
              + [nm + str(k) for nm in ("y0", "y1", "y2", "y3") for k in range(len(CHUNKS))])


def rank_program(g, core, T, topo):
    rank = T.rank_of(core)
    if rank is None:
        return
    V, S, P, Q = g.vector, g.scalar, g.tensor, g.sync
    add, sub, mn = AluOpType.add, AluOpType.subtract, AluOpType.min
    Copy, Ident = ActivationFunctionType.Copy, ActivationFunctionType.Identity
    base = H * rank
    mid = base + 1024
    total = {"ldM": 32, "dN": 32, "dH": 32, "out": 16 * (len(CHUNKS) + 1), "Wc": 4, "W1": 3, "NX": 8, "TR": 2, "D": 3}
    for nm in DMAS:
        total[nm] = 16
    for k in range(4):
        total["r%d" % k] = 2 * (N - 1)
        total["q%d" % k] = 2 * (N - 1)
    allA = ["A%d" % k for k in range(len(AX) - 1)]
    allG = ["G%d" % k for k in range(len(GP) - 1)]
    allAn = ["An%d" % k for k in range(len(AN) - 1)]
    allF = ["F%d" % k for k in range(len(AN) - 1)]
    allC = ["aC%d" % k for k in range(len(CC) - 1)]
    allY = ["aY%d" % k for k in range(len(YA) - 1)]
    allU = [nm for nm in G_ORDER.split() if nm[:2] == "aU"]
    Ub = T.A if allU else T.U
    allU = allU or ["yU%d" % k for k in range(4)]
    late = "cF2" in Q_ORDER.split()
    warm = "ldT" in G_ORDER.split()
    quarter = [(512 * k, 512 * (k + 1)) for k in range(4)]
    edges = [sum(CHUNKS[:k]) for k in range(len(CHUNKS) + 1)]
    pieces = [(edges[k], edges[k + 1]) for k in range(len(CHUNKS))]
    sums = [nm for nm in P_ORDER.split() if nm[0] == "m"]
    waited = []

    def cover(names, cuts, a, b):
        return [nm for k, nm in enumerate(names) if cuts[k] < b and cuts[k + 1] > a]

    def wait(q, *names):
        for nm in names:
            if not any(q is q2 and nm == nm2 for q2, nm2 in waited):
                waited.append((q, nm))
                q.wait_ge(T.sem[nm], total.get(nm, 1))

    def done(ins, nm, n=1):
        ins.then_inc(T.sem[nm], n)

    def exchange(k, src, dst, off, w):
        trs = []
        for d in range(1, N):
            q = (rank + d) % N
            i, j = q - (q > rank), rank - (rank > q)
            rid, pid, _ = topo.addr(T.cores[q])
            eng = topo.engines(core, T.cores[q])[2 * d - 2:2 * d]
            trs.append(RemoteDMATransfer(dst_ids=[DstId(rid=rid, pnc=pid)], dma_engine_mask=sum(1 << e for e in eng),
                                         remote_sem=T.sem["r%d" % k], src=src[:, w * i:w * (i + 1)],
                                         dst=dst[:, off + w * j:off + w * (j + 1)]))
        g.remote_dma_fused(trs, local_sem=T.sem["q%d" % k])

    Lt, Ln, Lp, Ls, Lu, Lnn = 0, 128, 256, 384, 512, 640
    far, pf, tpf, spf = T.FL[:, 0:6], T.PFL[:, 0:6], T.TSL[:, 0:6], T.TSL[:, 6:12]

    def lst(c0, a=0, b=H):
        return T.L[:, c0 + a // 16:c0 + b // 16]

    def ylane(c, a, b):
        return T.Y[:, 4 * a + c:4 * b:4]

    def span(nm):
        return (quarter if nm[1] == "U" else pieces)[int(nm[-1])]

    def bank(nm):
        a, b = span(nm)
        return T["PM%d" % (sums.index(nm) % 4)][:, 0:b - a]

    def q_step(nm):
        if nm[0] == "o":
            a, b = span(nm)
            wait(Q, *["y%d%s" % (c, nm[1]) for c in range(4)])
            done(Q.dma_start(T.y[:, 4 * a:4 * b], T.Y[:, 4 * a:4 * b]), "out", 16)
            return
        f2 = GP[2] if late else H
        need, moves = {
            "cC0": (cover(allA, AX, 0, CH), [(T.C[:, 0:CH], T.A[:, 0:CH])]),
            "cC1": (allA, [(T.C[:, CH:H], T.A[:, CH:H])]),
            "dSl": (["SR1"], [(T.NP[:, 384:512], T.SR[2::16, :])]),
            "dN": (["g2", "Fn"] + ["ldT"] * warm, [(T.SR[4::16, :], T.NP[:, 128:256]), (T.SR[1::16, :], T.NP[:, 0:128])]),
            "cF0": (["Fq"] if late else cover(allF, AN, 0, GP[1]), [(T.F2[:, 0:GP[1]], T.F[:, 0:GP[1]])]),
            "cF1": (["Fq"], [(T.F2[:, GP[1]:f2], T.F[:, GP[1]:f2])]),
            "cF2": (["Fq"], [(T.F2[:, GP[2]:H], T.F[:, GP[2]:H])]),
            "dH": (["TR"], [(T.MH[:, 0:128], T.TR[0::16, :]), (T.MH[:, 128:256], T.TR[4::16, :])]),
            "dTg": (["TR"], [(T.MS[:, 128:256], T.TR[1::16, :])]),
            "dSg": (["SR2"], [(T.MS[:, 0:128], T.SR[2::16, :])]),
            "nx": (["NX"], [(T.nx[:], T.NX[:])])}[nm]
        wait(Q, *need)
        for out, in_ in moves:
            done(Q.dma_start(out, in_), "out" if nm == "nx" else nm, 16)

    done(Q.dma_start(T.Mi[:, 0:128], T.twn[:]), "ldM", 16)
    done(Q.dma_start(T.Mi[:, 128:256], T.nxt[:]), "ldM", 16)
    done(Q.dma_start(T.X[:], T.x[:]), "ldx", 16)
    done(Q.dma_start(T.X2[:, 0:AX[1]], T.x[:, 0:AX[1]]), "ldX0", 16)
    wait(Q, "W0", "W1", "Wc", "Fp")
    done(Q.dma_start(T.W[2::16, :], T.NP[:, 256:384]), "ldP", 16)
    for k in range(1, len(allA)):
        done(Q.dma_start(T.X2[:, AX[k]:AX[k + 1]], T.x[:, AX[k]:AX[k + 1]]), "ldX%d" % k, 16)
    for nm in Q_ORDER.split():
        q_step(nm)
    wait(Q, "out")

    def g_copy(out, in_, n, nm):
        done(g.affine_select(out, in_, [[0, n]], AluOpType.is_equal, 0.0, 0, 0), nm)

    def g_add(out, in_, nm):
        done(g.dma_start(out, in_, accum_op=add), nm, 16)

    def g_step(nm):
        if nm == "J":
            done(g.iota(T.J[:], [[1, M]], 1024, 0, allow_small_or_imprecise_dtypes=True), nm)
        elif nm == "Zl":
            done(g.affine_select(T.Zl[:], T.oneb[:, 0:320], [[-2000, 2], [16, 10], [1001, 16]], AluOpType.is_equal, 0.0, -16, -1), nm)
        elif nm == "Id":
            wait(g, "two")
            done(g.affine_select(T.Id[:], T.oneb[:, 192:448], [[0, 2], [-1, 128]], AluOpType.is_equal, 0.0, 0, 1), nm)
        elif nm == "ldT":
            done(g.dma_start(T.NP[:, 0:128], T.twn[:]), nm, 16)
        elif nm == "ex0":
            wait(g, "s0")
            exchange(0, T.s0, T.l0, 0, E)
        elif nm == "ex1":
            wait(g, "s1")
            exchange(1, T.s1, T.A, H, E)
        elif nm == "ex2":
            wait(g, "s2a", "s2n")
            exchange(2, T.s2, T.l2, 0, 2 * E)
        elif nm == "ex3":
            wait(g, "s3")
            exchange(3, T.s3, T.G, H, E)
        elif nm == "g1":
            wait(g, "s0")
            g_copy(T.g1[:], T.s0[:], M, nm)
        elif nm == "hs":
            wait(g, "dSl", "Fp")
            g_copy(T.h16[:, 256:512], T.NP[:, 256:512], 256, nm)
        elif nm == "hh":
            wait(g, "dH")
            g_copy(T.h16[:, 512:768], T.MH[:], 256, nm)
        elif nm[:2] == "aC":
            a, b = CC[int(nm[2])], CC[int(nm[2]) + 1]
            wait(g, *(cover(["cC0", "cC1"], [0, CH, H], a, b) + cover(allAn, AN, a, b)))
            g_add(T.C[:, a:b], T.An[:, a:b], nm)
        elif nm[:2] == "aU":
            a, b = (0, H) if nm == "aU" else (CC[int(nm[2])], CC[int(nm[2]) + 1])
            wait(g, "s2a", "cC0", "cC1", *(cover(allC, CC, a, b) + allF))
            g_add(T.A[:, a:b], T.C[:, a:b], nm)
        elif nm[:2] == "aY":
            k0, k1 = YA[int(nm[2])], YA[int(nm[2]) + 1]
            a, b = edges[k0], edges[k1]
            wait(g, *(["p%d" % k for k in range(k0, k1)] + cover(allC, CC, a, b)))
            g_add(T.Y3[:, a:b], T.C[:, a:b], nm)
        else:
            k = int(nm[1])
            a, b = pieces[k]
            wait(g, *cover(allY, YA, k, k + 1))
            g_copy(ylane(3, a, b), T.Y3[:, a:b], b - a, "y3%d" % k)

    done(g.iota(T.W[:, 0:256], [[1, 256]], -1024, 0, allow_small_or_imprecise_dtypes=True), "W0")
    wait(g, "oneb")
    done(g.affine_select(T.Z0[:], T.oneb[:, 0:160], [[32, 5], [1000, 2], [1, 16]], AluOpType.is_equal, 0.0, -1000, -1), "Z0")
    done(g.affine_select(T.Z1[:], T.oneb[:, 0:160], [[32, 5], [1000, 2], [1, 16]], AluOpType.is_equal, 0.0, -16, -1), "Z1")
    for nm in G_ORDER.split():
        g_step(nm)
    wait(g, "q0", "q1", "q2", "q3")

    def to_list(ps, t0, ev):
        for s in range(8):
            b, u = s // 2, s % 2
            z = T.Z1 if u else T.Z0
            for g1 in range(2):
                o = 16 - 16 * (g1 - u)
                c = 32 * b + 16 * g1
                ins = P.matmul(ps[:, s:256:8], z[:, o:o + 128], T.T16[:, t0:t0 + 2, c:c + 16], g1 == 0, g1 == 1)
        done(ins, ev)

    def lane_to_list(ps, c0, lane, src):
        for i in range(16):
            ins = P.matmul(ps[:, c0:c0 + 6], T.Zl[:, 81 * lane + 16 - i:81 * lane + 144 - i], src[:, i:M:16], i == 0, i == 15)
        return ins

    def psum_add(ps, parts, twice=False):
        for k, part in enumerate(parts):
            c = 128 if twice and k == 0 else 0
            ins = P.matmul(ps, T.Id[:, c:c + 128], part, k == 0, k == len(parts) - 1)
        return ins

    def p_step(nm):
        if nm == "PF":
            wait(P, "g1", "Zl")
            done(lane_to_list(T.PF, 0, 2, T.g1), nm)
        elif nm == "PT":
            wait(P, "g2", "Zl")
            lane_to_list(T.PH, 0, 0, T.g2)
            done(lane_to_list(T.PH, 6, 2, T.g2), nm)
        elif nm == "PS":
            wait(P, "Ts")
            to_list(T.PG, 2, nm)
        elif nm == "PH":
            wait(P, "Id", "r1", "r2", "s2n", "PFL")
            psum_add(T.PF[:, 0:M], [T.A[:, H:H + M], T.l2[:, 1:2 * M:2]])
            done(psum_add(T.PF[:, M:2 * M], [T.A[:, H:H + M], T.s2[:, 1:2 * M:2], T.l2[:, 0:2 * M:2]]), nm)
        elif nm == "PU":
            wait(P, "Th", "Ltn")
            to_list(T.PL, 4, nm)
        else:
            a, b = span(nm)
            j = sums.index(nm)
            wait(P, "Id", *(["y" + sums[j - 4][1:]] if j >= 4 else []))
            if nm[1] == "U":
                wait(P, *cover(allAn, AN, a, b))
                done(psum_add(bank(nm), [T.A[:, a:b], T.An[:, a:b]], True), nm)
            elif nm[1] == "1":
                wait(P, "Fq", "u" + nm[2])
                done(psum_add(bank(nm), [T.F[:, a:b], T.Cu[:, a:b]]), nm)
            else:
                wait(P, "p" + nm[2], *cover(allC, CC, a, b))
                done(psum_add(bank(nm), [T.C[:, a:b], T.Y3[:, a:b]]), nm)

    wait(P, "T0", "Z0", "Z1")
    to_list(T.PL, 0, "PL")
    for nm in P_ORDER.split():
        p_step(nm)

    def nxop(k, src, c):
        done(S.activation(T.NX[:, k:1024:8], src, Ident, bias=float(c), scale=8.0), "NX")

    def s_step(nm):
        if nm == "s2n":
            wait(S, *allAn)
            done(S.activation(T.s2[:, 1:2 * M:2], T.An[:].indirect(far), Copy), nm)
        elif nm in ("TR0", "TR1"):
            a = 1024 * int(nm[2])
            wait(S, "dN")
            done(S.activation(T.TR[:, a:a + 1024], T.SR[:].indirect(lst(Ln, a, a + 1024)), Copy), "TR")
        elif nm == "Ch":
            wait(S, "PH")
            done(S.activation(T.C[:, H:H + 2 * M], T.PF[:, 0:2 * M], Copy), nm)
        elif nm == "nxu":
            wait(S, "dTg")
            nxop(2, T.MS[:, 128:256], 8 * mid * (1 - warm) + 6)
            nxop(7, T.MS[:, 128:256], 8 * mid * (1 - warm) + 5)
        elif nm == "nxs":
            wait(S, "dSg")
            nxop(4, T.MS[:, 0:128], 8 * mid + 4)
            nxop(5, T.MS[:, 0:128], 8 * mid + 3)
        else:
            a, b = span(nm)
            if nm[0] == "p":
                wait(S, "Fq", "Ls")
                done(S.activation(T.Y3[:, a:b], T.F[:, 0:H].indirect(lst(Lp, a, b)), Copy), nm)
            elif nm[0] == "u":
                wait(S, "Ch", "LU", *allC)
                done(S.activation(T.Cu[:, a:b], T.C[:, 0:H + M].indirect(lst(Lu, a, b)), Copy), nm)
            elif nm[0] == "e":
                wait(S, "m" + nm[1:])
                out = T.U[:, a:b] if nm[1] == "U" else ylane(int(nm[1]), a, b)
                done(S.activation(out, bank("m" + nm[1:]), Copy), "y" + nm[1:])
            else:
                wait(S, "r3", "Ls", *(["Gq"] if "Gq" in V_ORDER.split() else allG))
                done(S.activation(ylane(2, a, b), T.G[:].indirect(lst(Ls, a, b)), Copy), "y" + nm[1:])

    done(S.dma_start(T.Mi[:, 256:384], T.prv[:]), "ldp", 16)
    done(S.dma_start(T.fari[:, 0:6], T.far[:]), "ldf", 16)
    wait(S, "W0")
    for k in range(4, 8):
        done(S.activation(T.W[:, 256 * k:256 * (k + 1)], T.W[:, 0:256], Ident, bias=float(256 * k)), "Wc")
    wait(S, "Fp", "oneb")
    nxop(3, T.NP[:, 256:384], 8 * mid + 1)
    nxop(6, T.NP[:, 256:384], 8 * mid + 2)
    for i in range(N - 1):
        done(S.activation(T.D[:, E * i:E * (i + 1)], T.oneb[:, 0:E], Copy, scale=float(H * (i + (i >= rank) - rank))), "D")
    wait(S, "Fn")
    nxop(0, T.NP[:, 128:256], 8 * mid)
    nxop(1, T.NP[:, 128:256], 8 * mid + 7)
    wait(S, "ldP", "FL")
    done(S.activation(T.s0[:], T.W[:].indirect(far), Copy), "s0")
    wait(S, "Ltn")
    done(S.activation(T.SR[:], T.W[:].indirect(lst(Lt)), Copy), "SR")
    wait(S, *allA)
    for k, nm in enumerate(allAn):
        a, b = AN[k], AN[k + 1]
        done(S.activation(T.An[:, a:b], T.A[:, 0:H].indirect(lst(Ln, a, b)), Copy), nm)
    for nm in S_ORDER.split():
        s_step(nm)

    seen = []

    def v_step(nm):
        if nm == "g1":
            wait(V, "s0")
            done(V.tensor_copy(T.g1[:], T.s0[:]), nm)
        elif nm == "s1":
            wait(V, "FL", *allA)
            done(V.tensor_copy(T.s1[:], T.A[:, 0:H].indirect(far)), nm)
        elif nm == "PFL":
            wait(V, "PF")
            done(V.tensor_scalar(pf, T.PF[:, 0:6], 1024.0, None, add), nm)
        elif nm == "SR1":
            wait(V, "SR", "J")
            done(V.tensor_copy(T.SR[:].indirect(far), T.J[:]), nm)
        elif nm == "g2":
            wait(V, "SR1", "PFL")
            done(V.tensor_copy(T.g2[:], T.SR[:].indirect(pf)), nm)
        elif nm == "TSL":
            wait(V, "PT")
            done(V.tensor_scalar(T.TSL[:, 0:12], T.PH[:, 0:12], 1024.0, None, add), nm)
        elif nm == "s2a":
            wait(V, "r1", "TSL", "s1")
            done(V.tensor_tensor(T.s2[:, 0:2 * M:2], T.A[:].indirect(tpf), T.s1[:], add), nm)
        elif nm == "hs":
            wait(V, "dSl", "Fp")
            done(V.tensor_copy(T.h16[:, 256:512], T.NP[:, 256:512]), nm)
        elif nm == "Ts":
            wait(V, "hs")
            done(V.transpose(T.T16[:, 2:4, :], T.h16[:, 256:512]), nm)
        elif nm == "Ls":
            wait(V, "PS")
            done(V.tensor_scalar(T.L[:, Lp:Lp + 256], T.PG[:, 0:256], 1024.0, None, add), nm)
        elif nm == "Fq":
            wait(V, "r1", "s2n", *(allF + ([] if late else ["cF0"])))
            done(V.tensor_tensor(T.F[:, 0:H].indirect(far), T.s2[:, 1:2 * M:2], T.A[:, H:H + M], add), nm)
        elif nm == "s3":
            wait(V, "r2", "Fh", *seen)
            done(V.tensor_copy(T.F[:, H:H + M], T.l2[:, 0:2 * M:2]), "Fl")
            wait(V, "Fl", "Fq", "s2a")
            done(V.tensor_tensor(T.s3[:], T.F[:].indirect(spf), T.s2[:, 0:2 * M:2], add), nm)
        elif nm == "hh":
            wait(V, "dH")
            done(V.tensor_copy(T.h16[:, 512:768], T.MH[:]), nm)
        elif nm == "Th":
            wait(V, "hh")
            done(V.transpose(T.T16[:, 4:6, :], T.h16[:, 512:768]), nm)
        elif nm == "SR2":
            wait(V, "r0", "TR", "D", "dSl")
            done(V.tensor_tensor(T.SR[:].indirect(far), T.l0[:], T.D[:], add), nm)
        elif nm == "LU":
            wait(V, "PU")
            done(V.tensor_scalar(T.L[:, Lu:Lu + 256], T.PL[:, 0:256], 1024.0, None, add), nm)
        elif nm == "Gq":
            wait(V, "Ch", *allG)
            done(V.tensor_copy(T.G[:, 0:H].indirect(far), T.C[:, H + M:H + 2 * M]), nm)
        elif nm[0] == "A":
            k = int(nm[1])
            a, b = AX[k], AX[k + 1]
            wait(V, "ldX%d" % k)
            done(V.tensor_tensor(T.A[:, a:b], T.X[:].indirect(lst(Ln, a, b)), T.X2[:, a:b], add), nm)
        elif nm[0] == "F":
            k = int(nm[1])
            a, b = AN[k], AN[k + 1]
            wait(V, allAn[k])
            done(V.tensor_tensor(T.F[:, a:b], T.A[:, 0:H].indirect(lst(Lt, a, b)), T.An[:, a:b], add), nm)
        elif nm[0] == "G":
            k = int(nm[1])
            a, b = GP[k], GP[k + 1]
            wait(V, "Fq", "Ls", "Fh", *(["cF%d" % min(k, 2)] if late else ["cF1"] if k else []))
            done(V.tensor_tensor(T.G[:, a:b], T.F[:].indirect(lst(Ls, a, b)), T.F2[:, a:b], add), nm)
            seen.append(nm)
        else:
            a, b = span(nm)
            if nm[1] == "0":
                wait(V, "LU", *allU)
                win, c0, other = Ub[:, 0:H], Lnn, T.An
            elif nm[1] == "1":
                wait(V, "LU", "Ch", "Fq", *allC)
                win, c0, other = T.C[:, 0:H + M], Lu, T.F
            else:
                wait(V, "Ls", "Fq", *cover(allC, CC, a, b))
                win, c0, other = T.F[:, 0:H], Lp, T.C
            done(V.tensor_tensor(ylane(int(nm[1]), a, b), win.indirect(lst(c0, a, b)), other[:, a:b], add), "y" + nm[1:])

    done(V.memset(T.oneb[:, 0:320], 1.0), "oneb")
    done(V.memset(T.F[:, H:H + M], 0.0), "Fh")
    done(V.memset(T.oneb[:, 320:448], 2.0), "two")
    wait(V, "W0")
    for k in range(1, 4):
        done(V.tensor_scalar(T.W[:, 256 * k:256 * (k + 1)], T.W[:, 0:256], float(256 * k), None, add), "W1")
    wait(V, "ldp")
    done(V.tensor_scalar(T.NP[:, 256:384], T.Mi[:, 256:384], float(mid), None, sub), "Fp")
    wait(V, "ldM")
    done(V.tensor_scalar(T.h16[:, 0:256], T.Mi[:, 0:256], float(base), float(H - 1), sub, mn), "h0")
    wait(V, "h0")
    done(V.transpose(T.T16[:, 0:2, :], T.h16[:, 0:256]), "T0")
    wait(V, "ldf")
    done(V.tensor_copy(far, T.fari[:, 0:6]), "FL")
    done(V.tensor_scalar(T.NP[:, 128 * warm:256], T.Mi[:, 128 * warm:256], float(mid), None, sub), "Fn")
    wait(V, "PL")
    done(V.tensor_copy(T.L[:, 0:256], T.PL[:, 0:256]), "Ltn")
    wait(V, "Ltn", "ldx")
    for nm in V_ORDER.split():
        v_step(nm)
